import numpy as np
import ml_dtypes


def mxq(x, axis, fmt="e4m3"):
    dtype, down = {"e4m3": (ml_dtypes.float8_e4m3fn, 7), "e5m2": (ml_dtypes.float8_e5m2, 14)}[fmt]
    v = np.moveaxis(np.asarray(x, np.float32).astype(ml_dtypes.bfloat16).astype(np.float64), axis, -1)
    blocks = v.reshape(v.shape[:-1] + (-1, 32))
    amax = np.abs(blocks).max(-1, keepdims=True)
    byte = np.maximum(np.where(amax > 0, np.frexp(amax)[1] - 1 + 127, 0) - down, 1)
    scale = np.exp2(byte - 127.0)
    codes = (blocks / scale).astype(np.float32).astype(dtype).astype(np.float64)
    return np.moveaxis((codes * scale).reshape(v.shape), -1, axis)


WIDE = False


def mx_kscale(k):
    if not WIDE:
        return np.ones(k)
    levels = np.array([10, -10, 5, -5, 0])
    if k % 512:
        return np.exp2(np.random.permutation(np.resize(levels, k // 32))).repeat(32)
    a = np.empty((k // 512, 16))
    for p in range(k // 512):
        a[p, :8] = np.random.permutation(np.resize(levels, 8))
        for g in range(8):
            far = levels[np.abs(levels - a[p, g]) >= 10]
            a[p, g + 8] = far[np.random.randint(len(far))]
    return np.exp2(a.ravel()).repeat(32)


BF16 = ml_dtypes.bfloat16


def bf(x):
    return np.asarray(x, np.float32).astype(BF16)


def f64(x):
    return np.asarray(x).astype(np.float64)


T, V, D, CA, CB = 2048, 1024, 512, 1024, 512


def draw0():
    sa, sb = mx_kscale(CA), mx_kscale(CB)
    t = mx_kscale(T)
    ga = np.random.standard_normal((T, CA)) * sa
    wa = np.random.standard_normal((D, CA)) / np.sqrt(CA) / sa
    gb = np.random.standard_normal((T, CB)) * sb
    wb = np.random.standard_normal((CB, D)) / np.sqrt(CB) / sb[:, None]
    lam = np.random.uniform(0.5, 1.5, (T,))
    act = np.random.uniform(0.2, 1.0, (T, D)) * t[:, None]
    x = np.abs(np.random.standard_normal((T, V))) / np.sqrt(T) / t[:, None]
    return {"ga": bf(ga), "wa": bf(wa), "gb": bf(gb), "wb": bf(wb),
            "lam": bf(lam), "act": bf(act), "x": bf(x)}


def core(ga, wa, gb, wb, lam, act, x):
    pa = mxq(f64(ga), 1, "e4m3") @ mxq(f64(wa), 1, "e4m3").T
    pb = mxq(f64(gb), 1, "e4m3") @ mxq(f64(wb), 0, "e4m3")
    dz = (pa + f64(lam)[:, None] * pb) * f64(act)
    return mxq(f64(x), 0, "e4m3").T @ mxq(dz, 0, "e4m3")


def e4m3fn_bytes(y):
    return np.clip(np.asarray(y, np.float64), -448.0, 448.0).astype(np.float32).astype(ml_dtypes.float8_e4m3fn).view(np.uint8)


def e4m3fn_values(b):
    return np.asarray(b, np.uint8).view(ml_dtypes.float8_e4m3fn).astype(np.float64)


def setup_inputs():
    d = draw0()
    x0 = np.asarray(d['x']).astype(np.float64)
    s = (np.max(np.abs(x0), axis=(1,), keepdims=True) / 448.0).astype(np.float32)
    out = {}
    for k, v in d.items():
        if k == 'x':
            out['x_bytes'] = e4m3fn_bytes(x0 / s.astype(np.float64))
            out['x_scale'] = s
        else:
            out[k] = v
    return out


def reference(ga, wa, gb, wb, lam, act, x_bytes, x_scale):
    return core(ga, wa, gb, wb, lam, act, e4m3fn_values(x_bytes) * x_scale.astype(np.float64))

@@ -1,0 +1,322 @@
+from contextlib import ExitStack
+
+import concourse.mybir as mybir
+from concourse.masks import make_identity
+
+T, V, D, CA, CB = 2048, 1024, 512, 1024, 512
+FLOPS = 2 * T * D * CA + 2 * T * D * CB + 2 * V * D * T
+
+F32 = mybir.dt.float32
+BF16 = mybir.dt.bfloat16
+U32 = mybir.dt.uint32
+U8 = mybir.dt.uint8
+FP8 = mybir.dt.float8_e4m3fn
+FP8X4 = mybir.dt.float8_e4m3fn_x4
+COPY = mybir.ActivationFunctionType.Copy
+MULT = mybir.AluOpType.mult
+ADD = mybir.AluOpType.add
+
+P = 128
+G = T // 512
+PA_PASSES = CA // 512
+
+
+def tile_embedding_gradient_two_losses_s7_kernel(tc, ga, wa, gb, wb, lam, act, x_bytes, x_scale, out):
+    nc = tc.nc
+    with ExitStack() as ctx:
+        keep = ctx.enter_context(tc.tile_pool(name="keep", bufs=1))
+        work = ctx.enter_context(tc.tile_pool(name="work", bufs=2))
+        psum = ctx.enter_context(tc.psum_pool(name="psum", bufs=1))
+
+        def kt(name, shape, dt):
+            return keep.tile(shape, dt, name=name, tag=name, align_bytes=64)
+
+        def wt(name, shape, dt, bufs):
+            return work.tile(shape, dt, name=name, tag=name, bufs=bufs, align_bytes=64)
+
+        def bank(tag):
+            return psum.tile([P, 512], F32, name="bank_" + tag, tag=tag, bufs={"tr": 4, "pa": 2, "pb": 2}[tag])
+
+        xscale_sb = kt("xscale", [P, G, 4], F32)
+        nc.scalar.dma_start(out=xscale_sb[:], in_=x_scale.rearrange("(g p t) o -> p g (t o)", p=P, t=4))
+        lam_bf = kt("lam_bf", [P, G, 4], BF16)
+        nc.scalar.dma_start(out=lam_bf[:], in_=lam.rearrange("(g p t) -> p g t", p=P, t=4))
+
+        ident = kt("ident", [P, P], F32)
+        make_identity(nc, ident[:])
+
+        x_raw = [kt("x_raw%d" % g, [P, 4, V], U8) for g in range(G)]
+        x_view = x_bytes.rearrange("(g p t) n -> g p t n", p=P, t=4)
+        wa_sb = kt("wa_sb", [P, 4, CA], BF16)
+        wa_view = wa.rearrange("(j r) k -> j r k", r=P)
+        wb_sb = kt("wb_sb", [P, 4, D], BF16)
+        ga_sb = [kt("ga_sb%d" % g, [P, 4, CA], BF16) for g in range(G)]
+        gb_sb = [kt("gb_sb%d" % g, [P, 4, CB], BF16) for g in range(G)]
+        act_sb = [kt("act_sb%d" % g, [P, 4, D], BF16) for g in range(G)]
+        ga_view = ga.rearrange("(g p t) k -> g p t k", p=P, t=4)
+        gb_view = gb.rearrange("(g p t) k -> g p t k", p=P, t=4)
+        act_view = act.rearrange("(g p t) k -> g p t k", p=P, t=4)
+
+        def load_x(g):
+            nc.sync.dma_start(out=x_raw[g][:], in_=x_view[g])
+
+        def load_pair(tile, view, h):
+            nc.sync.dma_start(out=tile[:, 2 * h : 2 * h + 2, :], in_=view[:, 2 * h : 2 * h + 2, :])
+
+        for t in range(4):
+            nc.sync.dma_start(out=x_raw[0][:, t, :], in_=x_view[0][:, t, :])
+        for j in range(4):
+            nc.sync.dma_start(out=wa_sb[:, j, :], in_=wa_view[j])
+        load_pair(ga_sb[0], ga_view[0], 0)
+        load_pair(gb_sb[0], gb_view[0], 0)
+        nc.sync.dma_start(out=wb_sb[:], in_=wb.rearrange("(p t) d -> p t d", t=4))
+        load_pair(ga_sb[0], ga_view[0], 1)
+        load_pair(gb_sb[0], gb_view[0], 1)
+        nc.sync.dma_start(out=act_sb[0][:], in_=act_view[0])
+        load_x(1)
+        for g in range(1, G):
+            for h in range(2):
+                load_pair(ga_sb[g], ga_view[g], h)
+                load_pair(gb_sb[g], gb_view[g], h)
+            nc.sync.dma_start(out=act_sb[g][:], in_=act_view[g])
+            if g == 2:
+                load_x(2)
+        load_x(3)
+
+        lam_sb = kt("lam_sb", [P, G, 4], F32)
+        nc.gpsimd.tensor_copy(out=lam_sb[:], in_=lam_bf[:])
+
+        x_codes = [kt("x_codes%d" % g, [P, V], U32) for g in range(2)]
+        x_scales = [kt("x_scales%d" % g, [P, V], U8) for g in range(2)]
+        late_codes = kt("late_codes", [P, 2 * V], U32)
+        late_scales = kt("late_scales", [P, 2 * V], U8)
+        x_wide = {}
+        x_grp = {}
+
+        def widen(g, t, c0, c1, on_vector):
+            if g not in x_wide:
+                x_wide[g] = wt("x_wide", [P, 4, V], BF16, 3)
+            src = x_raw[g][:, t, c0:c1].bitcast(FP8)
+            dst = x_wide[g][:, t, c0:c1]
+            sc = xscale_sb[:, g, t : t + 1]
+            if on_vector:
+                nc.vector.tensor_scalar(out=dst, in0=src, scalar1=sc, scalar2=None, op0=MULT)
+            else:
+                nc.scalar.activation(out=dst, in_=src, func=COPY, scale=sc)
+
+        def interleave_x(g, c0, c1):
+            grp = wt("x_grp", [P, 512, 4], BF16, 3)
+            x_grp[g, c0] = grp
+            nc.vector.tensor_copy(
+                out=grp[:, : c1 - c0, :].rearrange("p (c i) t -> p c t i", i=4),
+                in_=x_wide[g][:, :, c0:c1].rearrange("p t (c i) -> p c t i", i=4),
+            )
+
+        def quantize_x(g, c0, c1):
+            nc.vector.quantize_mx(
+                out=x_codes[g][:, c0:c1].bitcast(FP8X4),
+                scales=x_scales[g][:, c0:c1],
+                in_=x_grp[g, c0][:, : c1 - c0, :].rearrange("p n t -> p (n t)"),
+            )
+
+        wa_grp = wt("sums", [P, 2, D, 4], BF16, 2)
+        wa_codes = kt("wa_codes", [P, 2, D], U32)
+        wa_scales = kt("wa_scales", [P, 2, D], U8)
+        wb_grp = wt("x_grp", [P, 512, 4], BF16, 3)
+        wb_codes = kt("wb_codes", [P, D], U32)
+        wb_scales = kt("wb_scales", [P, D], U8)
+
+        def transpose_words(dst, words, passes):
+            for c in range(passes):
+                for u in range(2):
+                    nc.tensor.transpose(dst[:, c, u, :], words[:, 256 * c + u : 256 * (c + 1) : 2], ident[:])
+
+        def wa_rows(j):
+            b = bank("tr")
+            bv = b[:].rearrange("p (c u r) -> p c u r", c=2, u=2)
+            transpose_words(bv, wa_sb[:, j, :].bitcast(F32), 2)
+            nc.scalar.copy(
+                out=wa_grp[:, :, P * j : P * (j + 1), :].rearrange("p c r t -> p c (r t)").bitcast(F32).rearrange("p c (r u) -> p c r u", u=2),
+                in_=bv.rearrange("p c u r -> p c r u"),
+            )
+
+        def quantize_wa(c):
+            nc.vector.quantize_mx(out=wa_codes[:, c, :].bitcast(FP8X4), scales=wa_scales[:, c, :], in_=wa_grp[:, c, :, :].rearrange("p d t -> p (d t)"))
+
+        def interleave_wb():
+            nc.vector.tensor_copy(out=wb_grp[:].rearrange("p (c i) t -> p c t i", i=4), in_=wb_sb[:].rearrange("p t (c i) -> p c t i", i=4))
+
+        def quantize_wb():
+            nc.vector.quantize_mx(out=wb_codes[:].bitcast(FP8X4), scales=wb_scales[:], in_=wb_grp[:].rearrange("p d t -> p (d t)"))
+
+        a_grp, b_grp, a_q, b_q = {}, {}, {}, {}
+
+        def prep(s):
+            g, h = s // 2, s % 2
+            a_grp[s] = wt("a_grp", [P, 2, 2, P, 4], BF16, 2)
+            b_grp[s] = wt("b_grp", [P, 2, P, 4], BF16, 2)
+            for i in range(2):
+                b = bank("tr")
+                bv = b[:].rearrange("p (c u r) -> p c u r", c=2, u=2)
+                transpose_words(bv, ga_sb[g][:, 2 * h + i, :].bitcast(F32), 2)
+                nc.scalar.copy(
+                    out=a_grp[s][:, i, :, :, :].rearrange("p c r t -> p (c r t)").bitcast(F32).rearrange("p (c r u) -> p c r u", c=2, u=2),
+                    in_=bv.rearrange("p c u r -> p c r u"),
+                )
+            b = bank("tr")
+            bv = b[:].rearrange("p (i u r) -> p i u r", i=2, u=2)
+            for i in range(2):
+                transpose_words(bv[:, i : i + 1, :, :], gb_sb[g][:, 2 * h + i, :].bitcast(F32), 1)
+            nc.scalar.copy(
+                out=b_grp[s][:].rearrange("p i r t -> p (i r t)").bitcast(F32).rearrange("p (i r u) -> p i r u", i=2, u=2),
+                in_=bv.rearrange("p i u r -> p i r u"),
+            )
+
+        def quantize_ab(s):
+            ac = wt("a_codes", [P, 2, 2, P], U32, 3)
+            asc = wt("a_scales", [P, 2, 2, P], U8, 3)
+            bc = wt("b_codes", [P, 2, P], U32, 3)
+            bsc = wt("b_scales", [P, 2, P], U8, 3)
+            nc.vector.quantize_mx(
+                out=ac[:].rearrange("p i c r -> p (i c r)").bitcast(FP8X4),
+                scales=asc[:].rearrange("p i c r -> p (i c r)"),
+                in_=a_grp[s][:].rearrange("p i c r t -> p (i c r t)"),
+            )
+            nc.vector.quantize_mx(
+                out=bc[:].rearrange("p i r -> p (i r)").bitcast(FP8X4),
+                scales=bsc[:].rearrange("p i r -> p (i r)"),
+                in_=b_grp[s][:].rearrange("p i r t -> p (i r t)"),
+            )
+            a_q[s] = (ac, asc)
+            b_q[s] = (bc, bsc)
+
+        pas, pbs = {}, {}
+
+        def products(s):
+            ac, asc = a_q[s]
+            bc, bsc = b_q[s]
+            for i in range(2):
+                pb = bank("pb")
+                nc.tensor.matmul_mx(
+                    out=pb[:], lhsT=bc[:, i, :].bitcast(FP8X4), lhsT_scale=bsc[:, i, :],
+                    rhs=wb_codes[:].bitcast(FP8X4), rhs_scale=wb_scales[:], start=True, stop=True,
+                )
+                pa = bank("pa")
+                for c in range(2):
+                    nc.tensor.matmul_mx(
+                        out=pa[:], lhsT=ac[:, i, c, :].bitcast(FP8X4), lhsT_scale=asc[:, i, c, :],
+                        rhs=wa_codes[:, c, :].bitcast(FP8X4), rhs_scale=wa_scales[:, c, :], start=(c == 0), stop=(c == 1),
+                    )
+                pas[s, i], pbs[s, i] = pa, pb
+
+        sums = {}
+
+        def combine(s):
+            g, h = s // 2, s % 2
+            if g not in sums:
+                sums[g] = wt("sums", [P, 4, D], F32, 2)
+            for i in range(2):
+                t = 2 * h + i
+                q = wt("lam_pb", [P, D], F32, 3)
+                nc.scalar.activation(out=q[:], in_=pbs[s, i][:], func=COPY, scale=lam_sb[:, g, t : t + 1])
+                nc.vector.tensor_tensor(out=sums[g][:, t, :], in0=pas[s, i][:], in1=q[:], op=ADD)
+
+        dz_codes = [kt("dz_codes%d" % g, [P, D], U32) for g in range(G)]
+        dz_scales = [kt("dz_scales%d" % g, [P, D], U8) for g in range(G)]
+        dz_grp = {}
+
+        def times_act(g, c0, c1):
+            grp = wt("dz_grp", [P, 512, 4], BF16, 2)
+            dz_grp[g, c0] = grp
+            nc.vector.tensor_tensor(
+                out=grp[:, : c1 - c0, :].rearrange("p (c i) t -> p c t i", i=4),
+                in0=sums[g][:, :, c0:c1].rearrange("p t (c i) -> p c t i", i=4),
+                in1=act_sb[g][:, :, c0:c1].rearrange("p t (c i) -> p c t i", i=4),
+                op=MULT,
+            )
+
+        def quantize_dz(g, c0, c1):
+            nc.vector.quantize_mx(
+                out=dz_codes[g][:, c0:c1].bitcast(FP8X4), scales=dz_scales[g][:, c0:c1],
+                in_=dz_grp[g, c0][:, : c1 - c0, :].rearrange("p n t -> p (n t)"),
+            )
+
+        for t in range(4):
+            widen(0, t, 0, V, t < 3)
+        for j in range(4):
+            wa_rows(j)
+        interleave_x(0, 0, 512)
+        quantize_wa(0)
+        quantize_wa(1)
+        prep(0)
+        interleave_x(0, 512, 1024)
+        quantize_x(0, 0, 512)
+        quantize_ab(0)
+        interleave_wb()
+        quantize_x(0, 512, 1024)
+        quantize_wb()
+        prep(1)
+
+        widen_at = {0: [(1, 0), (1, 1)], 1: [(1, 2), (1, 3)], 3: [(2, 0)], 4: [(2, 1)], 5: [(2, 2)], 6: [(2, 3)]}
+        inter_at = {2: (1, 0), 3: (1, 512)}
+        quant_at = {3: (1, 0), 4: (1, 512)}
+        for s in range(8):
+            g, h = s // 2, s % 2
+            products(s)
+            if s + 2 < 8:
+                prep(s + 2)
+            if s + 1 < 8:
+                quantize_ab(s + 1)
+            for gg, t in widen_at.get(s, []):
+                widen(gg, t, 0, V, False)
+            if s in inter_at:
+                gg, c0 = inter_at[s]
+                interleave_x(gg, c0, c0 + 512)
+            combine(s)
+            if s in quant_at:
+                gg, c0 = quant_at[s]
+                quantize_x(gg, c0, c0 + 512)
+            if h == 1:
+                parts = [(0, 512)] if g < 3 else [(0, 256), (256, 512)]
+                for c0, c1 in parts:
+                    times_act(g, c0, c1)
+                for c0, c1 in parts:
+                    quantize_dz(g, c0, c1)
+
+        tags = ["tr", "tr", "tr", "tr", "pa", "pb", "pa", "pb"]
+        chunks = [(0, 256), (256, 512), (512, 768), (768, 896), (896, 1024)]
+        for t in range(4):
+            widen(3, t, 0, 256, False)
+        for n, (c0, c1) in enumerate(chunks):
+            w = c1 - c0
+            grp = wt("x_grp", [P, 512, 4], BF16, 3)
+            for i in range(2):
+                nc.vector.tensor_copy(
+                    out=grp[:, i * w : (i + 1) * w, :].rearrange("p (c i) t -> p c t i", i=4),
+                    in_=x_wide[2 + i][:, :, c0:c1].rearrange("p t (c i) -> p c t i", i=4),
+                )
+            codes = late_codes[:, 2 * c0 : 2 * c1]
+            scales = late_scales[:, 2 * c0 : 2 * c1]
+            nc.vector.quantize_mx(out=codes.bitcast(FP8X4), scales=scales, in_=grp[:, : 2 * w, :].rearrange("p n t -> p (n t)"))
+            if n + 1 < len(chunks):
+                for t in range(4):
+                    widen(3, t, chunks[n + 1][0], chunks[n + 1][1], False)
+            for v in range(c0 // P, c1 // P):
+                acc = bank(tags[v])
+                cols = slice(P * v, P * (v + 1))
+                for g in range(G):
+                    if g < 2:
+                        lc, ls = x_codes[g][:, cols], x_scales[g][:, cols]
+                    else:
+                        o = (g - 2) * w + P * v - c0
+                        lc, ls = codes[:, o : o + P], scales[:, o : o + P]
+                    nc.tensor.matmul_mx(
+                        out=acc[:], lhsT=lc.bitcast(FP8X4), lhsT_scale=ls,
+                        rhs=dz_codes[g][:].bitcast(FP8X4), rhs_scale=dz_scales[g][:], start=(g == 0), stop=(g == G - 1),
+                    )
+                res = wt("res", [P, D], F32, 4)
+                if v < 7:
+                    nc.scalar.copy(out=res[:], in_=acc[:])
+                else:
+                    nc.vector.tensor_copy(out=res[:], in_=acc[:])
+                nc.sync.dma_start(out=out[cols, :], in_=res[:])

@@ -35,7 +35,7 @@ def tile_embedding_gradient_two_losses_s7_kernel(tc, ga, wa, gb, wb, lam, act, x
             return work.tile(shape, dt, name=name, tag=name, bufs=bufs, align_bytes=64)
 
         def bank(tag):
-            return psum.tile([P, 512], F32, name="bank_" + tag, tag=tag, bufs={"tr": 4, "pa": 2, "pb": 2}[tag])
+            return psum.tile([P, 512], F32, name="bank_" + tag, tag=tag, bufs={"tr": 3, "pa": 3, "pb": 2}[tag])
 
         xscale_sb = kt("xscale", [P, G, 4], F32)
         nc.scalar.dma_start(out=xscale_sb[:], in_=x_scale.rearrange("(g p t) o -> p g (t o)", p=P, t=4))
@@ -72,24 +72,20 @@ def tile_embedding_gradient_two_losses_s7_kernel(tc, ga, wa, gb, wb, lam, act, x
         nc.sync.dma_start(out=wb_sb[:], in_=wb.rearrange("(p t) d -> p t d", t=4))
         load_pair(ga_sb[0], ga_view[0], 1)
         load_pair(gb_sb[0], gb_view[0], 1)
-        nc.sync.dma_start(out=act_sb[0][:], in_=act_view[0])
-        load_x(1)
         for g in range(1, G):
-            for h in range(2):
-                load_pair(ga_sb[g], ga_view[g], h)
-                load_pair(gb_sb[g], gb_view[g], h)
-            nc.sync.dma_start(out=act_sb[g][:], in_=act_view[g])
-            if g == 2:
-                load_x(2)
-        load_x(3)
+            load_pair(ga_sb[g], ga_view[g], 0)
+            load_pair(gb_sb[g], gb_view[g], 0)
+            load_x(g)
+            load_pair(ga_sb[g], ga_view[g], 1)
+            load_pair(gb_sb[g], gb_view[g], 1)
+            nc.sync.dma_start(out=act_sb[g - 1][:], in_=act_view[g - 1])
+        nc.sync.dma_start(out=act_sb[3][:], in_=act_view[3])
 
         lam_sb = kt("lam_sb", [P, G, 4], F32)
         nc.gpsimd.tensor_copy(out=lam_sb[:], in_=lam_bf[:])
 
-        x_codes = [kt("x_codes%d" % g, [P, V], U32) for g in range(2)]
-        x_scales = [kt("x_scales%d" % g, [P, V], U8) for g in range(2)]
-        late_codes = kt("late_codes", [P, 2 * V], U32)
-        late_scales = kt("late_scales", [P, 2 * V], U8)
+        x_codes = [kt("x_codes%d" % g, [P, V], U32) for g in range(G)]
+        x_scales = [kt("x_scales%d" % g, [P, V], U8) for g in range(G)]
         x_wide = {}
         x_grp = {}
 
@@ -104,10 +100,10 @@ def tile_embedding_gradient_two_losses_s7_kernel(tc, ga, wa, gb, wb, lam, act, x
             else:
                 nc.scalar.activation(out=dst, in_=src, func=COPY, scale=sc)
 
-        def interleave_x(g, c0, c1):
-            grp = wt("x_grp", [P, 512, 4], BF16, 3)
+        def interleave_x(g, c0, c1, on_scalar=False):
+            grp = wt("x_grp", [P, 512, 4], BF16, 4)
             x_grp[g, c0] = grp
-            nc.vector.tensor_copy(
+            (nc.scalar.copy if on_scalar else nc.vector.tensor_copy)(
                 out=grp[:, : c1 - c0, :].rearrange("p (c i) t -> p c t i", i=4),
                 in_=x_wide[g][:, :, c0:c1].rearrange("p t (c i) -> p c t i", i=4),
             )
@@ -122,7 +118,7 @@ def tile_embedding_gradient_two_losses_s7_kernel(tc, ga, wa, gb, wb, lam, act, x
         wa_grp = wt("sums", [P, 2, D, 4], BF16, 2)
         wa_codes = kt("wa_codes", [P, 2, D], U32)
         wa_scales = kt("wa_scales", [P, 2, D], U8)
-        wb_grp = wt("x_grp", [P, 512, 4], BF16, 3)
+        wb_grp = wt("x_grp", [P, 512, 4], BF16, 4)
         wb_codes = kt("wb_codes", [P, D], U32)
         wb_scales = kt("wb_scales", [P, D], U8)
 
@@ -131,10 +127,13 @@ def tile_embedding_gradient_two_losses_s7_kernel(tc, ga, wa, gb, wb, lam, act, x
                 for u in range(2):
                     nc.tensor.transpose(dst[:, c, u, :], words[:, 256 * c + u : 256 * (c + 1) : 2], ident[:])
 
-        def wa_rows(j):
+        def wa_turn(j):
             b = bank("tr")
-            bv = b[:].rearrange("p (c u r) -> p c u r", c=2, u=2)
-            transpose_words(bv, wa_sb[:, j, :].bitcast(F32), 2)
+            banks["wa", j] = b
+            transpose_words(b[:].rearrange("p (c u r) -> p c u r", c=2, u=2), wa_sb[:, j, :].bitcast(F32), 2)
+
+        def wa_empty(j):
+            bv = banks["wa", j][:].rearrange("p (c u r) -> p c u r", c=2, u=2)
             nc.scalar.copy(
                 out=wa_grp[:, :, P * j : P * (j + 1), :].rearrange("p c r t -> p c (r t)").bitcast(F32).rearrange("p c (r u) -> p c r u", u=2),
                 in_=bv.rearrange("p c u r -> p c r u"),
@@ -151,75 +150,90 @@ def tile_embedding_gradient_two_losses_s7_kernel(tc, ga, wa, gb, wb, lam, act, x
 
         a_grp, b_grp, a_q, b_q = {}, {}, {}, {}
 
-        def prep(s):
+        banks = {}
+
+        def turn(s):
             g, h = s // 2, s % 2
-            a_grp[s] = wt("a_grp", [P, 2, 2, P, 4], BF16, 2)
-            b_grp[s] = wt("b_grp", [P, 2, P, 4], BF16, 2)
             for i in range(2):
                 b = bank("tr")
-                bv = b[:].rearrange("p (c u r) -> p c u r", c=2, u=2)
-                transpose_words(bv, ga_sb[g][:, 2 * h + i, :].bitcast(F32), 2)
-                nc.scalar.copy(
-                    out=a_grp[s][:, i, :, :, :].rearrange("p c r t -> p (c r t)").bitcast(F32).rearrange("p (c r u) -> p c r u", c=2, u=2),
-                    in_=bv.rearrange("p c u r -> p c r u"),
-                )
+                banks[s, i] = b
+                transpose_words(b[:].rearrange("p (c u r) -> p c u r", c=2, u=2), ga_sb[g][:, 2 * h + i, :].bitcast(F32), 2)
             b = bank("tr")
+            banks[s, 2] = b
             bv = b[:].rearrange("p (i u r) -> p i u r", i=2, u=2)
             for i in range(2):
                 transpose_words(bv[:, i : i + 1, :, :], gb_sb[g][:, 2 * h + i, :].bitcast(F32), 1)
-            nc.scalar.copy(
-                out=b_grp[s][:].rearrange("p i r t -> p (i r t)").bitcast(F32).rearrange("p (i r u) -> p i r u", i=2, u=2),
-                in_=bv.rearrange("p i u r -> p i r u"),
-            )
 
-        def quantize_ab(s):
+        def empty(s, i, on_vector=False):
+            if i == 0:
+                a_grp[s] = wt("a_grp", [P, 2, 2, P, 4], BF16, 2)
+            if i == 2:
+                b_grp[s] = wt("b_grp", [P, 2, P, 4], BF16, 2)
+            if i < 2:
+                dst = a_grp[s][:, i, :, :, :].rearrange("p c r t -> p (c r t)")
+            else:
+                dst = b_grp[s][:].rearrange("p i r t -> p (i r t)")
+            dst = dst.bitcast(F32).rearrange("p (c r u) -> p c r u", c=2, u=2)
+            src = banks[s, i][:].rearrange("p (c u r) -> p c r u", c=2, u=2)
+            if on_vector:
+                nc.vector.tensor_copy(out=dst, in_=src)
+            else:
+                nc.scalar.copy(out=dst, in_=src)
+
+        def quantize_a(s):
             ac = wt("a_codes", [P, 2, 2, P], U32, 3)
             asc = wt("a_scales", [P, 2, 2, P], U8, 3)
-            bc = wt("b_codes", [P, 2, P], U32, 3)
-            bsc = wt("b_scales", [P, 2, P], U8, 3)
             nc.vector.quantize_mx(
                 out=ac[:].rearrange("p i c r -> p (i c r)").bitcast(FP8X4),
                 scales=asc[:].rearrange("p i c r -> p (i c r)"),
                 in_=a_grp[s][:].rearrange("p i c r t -> p (i c r t)"),
             )
+            a_q[s] = (ac, asc)
+
+        def quantize_b(s):
+            bc = wt("b_codes", [P, 2, P], U32, 3)
+            bsc = wt("b_scales", [P, 2, P], U8, 3)
             nc.vector.quantize_mx(
                 out=bc[:].rearrange("p i r -> p (i r)").bitcast(FP8X4),
                 scales=bsc[:].rearrange("p i r -> p (i r)"),
                 in_=b_grp[s][:].rearrange("p i r t -> p (i r t)"),
             )
-            a_q[s] = (ac, asc)
             b_q[s] = (bc, bsc)
 
         pas, pbs = {}, {}
 
-        def products(s):
+        def products(k):
+            s, i = k // 2, k % 2
             ac, asc = a_q[s]
             bc, bsc = b_q[s]
-            for i in range(2):
-                pb = bank("pb")
+            pb = bank("pb")
+            nc.tensor.matmul_mx(
+                out=pb[:], lhsT=bc[:, i, :].bitcast(FP8X4), lhsT_scale=bsc[:, i, :],
+                rhs=wb_codes[:].bitcast(FP8X4), rhs_scale=wb_scales[:], start=True, stop=True,
+            )
+            pa = bank("pa")
+            for c in range(2):
                 nc.tensor.matmul_mx(
-                    out=pb[:], lhsT=bc[:, i, :].bitcast(FP8X4), lhsT_scale=bsc[:, i, :],
-                    rhs=wb_codes[:].bitcast(FP8X4), rhs_scale=wb_scales[:], start=True, stop=True,
+                    out=pa[:], lhsT=ac[:, i, c, :].bitcast(FP8X4), lhsT_scale=asc[:, i, c, :],
+                    rhs=wa_codes[:, c, :].bitcast(FP8X4), rhs_scale=wa_scales[:, c, :], start=(c == 0), stop=(c == 1),
                 )
-                pa = bank("pa")
-                for c in range(2):
-                    nc.tensor.matmul_mx(
-                        out=pa[:], lhsT=ac[:, i, c, :].bitcast(FP8X4), lhsT_scale=asc[:, i, c, :],
-                        rhs=wa_codes[:, c, :].bitcast(FP8X4), rhs_scale=wa_scales[:, c, :], start=(c == 0), stop=(c == 1),
-                    )
-                pas[s, i], pbs[s, i] = pa, pb
+            pas[k], pbs[k] = pa, pb
 
         sums = {}
 
-        def combine(s):
-            g, h = s // 2, s % 2
+        lam_pb = {}
+
+        def weigh(k):
+            g, t = k // 4, k % 4
+            q = wt("row", [P, D], F32, 4)
+            lam_pb[k] = q
+            nc.scalar.activation(out=q[:], in_=pbs[k][:], func=COPY, scale=lam_sb[:, g, t : t + 1])
+
+        def add(k):
+            g, t = k // 4, k % 4
             if g not in sums:
                 sums[g] = wt("sums", [P, 4, D], F32, 2)
-            for i in range(2):
-                t = 2 * h + i
-                q = wt("lam_pb", [P, D], F32, 3)
-                nc.scalar.activation(out=q[:], in_=pbs[s, i][:], func=COPY, scale=lam_sb[:, g, t : t + 1])
-                nc.vector.tensor_tensor(out=sums[g][:, t, :], in0=pas[s, i][:], in1=q[:], op=ADD)
+            nc.vector.tensor_tensor(out=sums[g][:, t, :], in0=pas[k][:], in1=lam_pb[k][:], op=ADD)
 
         dz_codes = [kt("dz_codes%d" % g, [P, D], U32) for g in range(G)]
         dz_scales = [kt("dz_scales%d" % g, [P, D], U8) for g in range(G)]
@@ -241,82 +255,105 @@ def tile_embedding_gradient_two_losses_s7_kernel(tc, ga, wa, gb, wb, lam, act, x
                 in_=dz_grp[g, c0][:, : c1 - c0, :].rearrange("p n t -> p (n t)"),
             )
 
-        for t in range(4):
-            widen(0, t, 0, V, t < 3)
-        for j in range(4):
-            wa_rows(j)
-        interleave_x(0, 0, 512)
-        quantize_wa(0)
-        quantize_wa(1)
-        prep(0)
-        interleave_x(0, 512, 1024)
-        quantize_x(0, 0, 512)
-        quantize_ab(0)
-        interleave_wb()
-        quantize_x(0, 512, 1024)
-        quantize_wb()
-        prep(1)
+        tags = ["tr", "tr", "tr", "pa", "pb", "pa", "pb", "pa"]
+        accs = {}
 
-        widen_at = {0: [(1, 0), (1, 1)], 1: [(1, 2), (1, 3)], 3: [(2, 0)], 4: [(2, 1)], 5: [(2, 2)], 6: [(2, 3)]}
-        inter_at = {2: (1, 0), 3: (1, 512)}
-        quant_at = {3: (1, 0), 4: (1, 512)}
-        for s in range(8):
-            g, h = s // 2, s % 2
-            products(s)
-            if s + 2 < 8:
-                prep(s + 2)
-            if s + 1 < 8:
-                quantize_ab(s + 1)
-            for gg, t in widen_at.get(s, []):
-                widen(gg, t, 0, V, False)
-            if s in inter_at:
-                gg, c0 = inter_at[s]
-                interleave_x(gg, c0, c0 + 512)
-            combine(s)
-            if s in quant_at:
-                gg, c0 = quant_at[s]
-                quantize_x(gg, c0, c0 + 512)
-            if h == 1:
-                parts = [(0, 512)] if g < 3 else [(0, 256), (256, 512)]
-                for c0, c1 in parts:
-                    times_act(g, c0, c1)
-                for c0, c1 in parts:
-                    quantize_dz(g, c0, c1)
+        def grad(v, g):
+            if v not in accs:
+                accs[v] = bank(tags[v])
+            cols = slice(P * v, P * (v + 1))
+            nc.tensor.matmul_mx(
+                out=accs[v][:], lhsT=x_codes[g][:, cols].bitcast(FP8X4), lhsT_scale=x_scales[g][:, cols],
+                rhs=dz_codes[g][:].bitcast(FP8X4), rhs_scale=dz_scales[g][:], start=(g == 0), stop=(g == G - 1),
+            )
 
-        tags = ["tr", "tr", "tr", "tr", "pa", "pb", "pa", "pb"]
-        chunks = [(0, 256), (256, 512), (512, 768), (768, 896), (896, 1024)]
-        for t in range(4):
-            widen(3, t, 0, 256, False)
-        for n, (c0, c1) in enumerate(chunks):
-            w = c1 - c0
-            grp = wt("x_grp", [P, 512, 4], BF16, 3)
-            for i in range(2):
-                nc.vector.tensor_copy(
-                    out=grp[:, i * w : (i + 1) * w, :].rearrange("p (c i) t -> p c t i", i=4),
-                    in_=x_wide[2 + i][:, :, c0:c1].rearrange("p t (c i) -> p c t i", i=4),
-                )
-            codes = late_codes[:, 2 * c0 : 2 * c1]
-            scales = late_scales[:, 2 * c0 : 2 * c1]
-            nc.vector.quantize_mx(out=codes.bitcast(FP8X4), scales=scales, in_=grp[:, : 2 * w, :].rearrange("p n t -> p (n t)"))
-            if n + 1 < len(chunks):
-                for t in range(4):
-                    widen(3, t, chunks[n + 1][0], chunks[n + 1][1], False)
-            for v in range(c0 // P, c1 // P):
-                acc = bank(tags[v])
-                cols = slice(P * v, P * (v + 1))
-                for g in range(G):
-                    if g < 2:
-                        lc, ls = x_codes[g][:, cols], x_scales[g][:, cols]
-                    else:
-                        o = (g - 2) * w + P * v - c0
-                        lc, ls = codes[:, o : o + P], scales[:, o : o + P]
-                    nc.tensor.matmul_mx(
-                        out=acc[:], lhsT=lc.bitcast(FP8X4), lhsT_scale=ls,
-                        rhs=dz_codes[g][:].bitcast(FP8X4), rhs_scale=dz_scales[g][:], start=(g == 0), stop=(g == G - 1),
-                    )
-                res = wt("res", [P, D], F32, 4)
-                if v < 7:
-                    nc.scalar.copy(out=res[:], in_=acc[:])
-                else:
-                    nc.vector.tensor_copy(out=res[:], in_=acc[:])
-                nc.sync.dma_start(out=out[cols, :], in_=res[:])
+        def finish(v, on_vector):
+            if v % 4 == 0:
+                sums["out", v // 4] = wt("sums", [P, 4, D], F32, 2)
+            res = sums["out", v // 4][:, v % 4, :]
+            if on_vector:
+                nc.vector.tensor_copy(out=res, in_=accs[v][:])
+            else:
+                nc.scalar.copy(out=res, in_=accs[v][:])
+            nc.sync.dma_start(out=out[P * v : P * (v + 1), :], in_=res)
+
+        with tc.manual_schedule():
+            W, S = True, False
+            for t in range(4):
+                widen(0, t, 0, V, t != 3)
+            for j in range(4):
+                wa_turn(j)
+                wa_empty(j)
+            interleave_x(0, 0, 512)
+            turn(0)
+            empty(0, 0); empty(0, 1); empty(0, 2)
+            interleave_x(0, 512, 1024)
+            quantize_wa(0)
+            quantize_wa(1)
+            interleave_wb()
+            quantize_a(0)
+            quantize_wb()
+            quantize_b(0)
+            turn(1)
+            empty(1, 0); empty(1, 1); empty(1, 2)
+            dve = {k: [] for k in range(20)}
+            act = {k: [] for k in range(20)}
+            for k in range(16):
+                s = k // 2
+                if k % 2 == 0 and s + 1 < 8:
+                    dve[k].append(lambda s=s: quantize_a(s + 1))
+                    dve[k].append(lambda s=s: quantize_b(s + 1))
+            dve[0].insert(0, lambda: quantize_x(0, 0, 512))
+            dve[1].insert(0, lambda: quantize_x(0, 512, 1024))
+            for i in range(4):
+                dve[1 + i // 2].append(lambda i=i: widen(1, i, 0, V, W))
+                act[4 + i].append(lambda i=i: widen(2, i, 0, V, S))
+                act[8 + i].append(lambda i=i: widen(3, i, 0, V, S))
+                act[12 + i].append(lambda i=i: interleave_x(3, 256 * i, 256 * i + 256, True))
+            for i, c in enumerate((0, 512)):
+                dve[3 + i].append(lambda c=c: interleave_x(1, c, c + 512))
+                dve[4 + 2 * i].insert(0, lambda c=c: quantize_x(1, c, c + 512))
+                dve[9 + 2 * i].append(lambda c=c: interleave_x(2, c, c + 512))
+                dve[10 + 2 * i].append(lambda c=c: quantize_x(2, c, c + 512))
+            for g in range(3):
+                dve[4 * g + 4].append(lambda g=g: times_act(g, 0, 256))
+                dve[4 * g + 5].append(lambda g=g: times_act(g, 256, 512))
+                dve[4 * g + 5].append(lambda g=g: quantize_dz(g, 0, 256))
+                dve[4 * g + 6].append(lambda g=g: quantize_dz(g, 256, 512))
+            dve[14].append(lambda: quantize_x(3, 0, 256))
+            dve[15].append(lambda: quantize_x(3, 256, 512))
+
+            for k in range(16):
+                s = k // 2
+                products(k)
+                if k % 2 == 0 and s + 2 < 8:
+                    turn(s + 2)
+                if k >= 13:
+                    grad(k - 13, 0)
+                    grad(k - 13, 1)
+                weigh(k)
+                if s + 2 < 8:
+                    for i in ((0, 1) if k % 2 == 0 else (2,)):
+                        empty(s + 2, i)
+                for f in act[k]:
+                    f()
+                for f in dve[k]:
+                    f()
+                add(k)
+            for v in range(3):
+                grad(v, 2)
+            for v in range(3, 8):
+                for g in range(3):
+                    grad(v, g)
+            times_act(3, 0, 256)
+            times_act(3, 256, 512)
+            quantize_dz(3, 0, 256)
+            quantize_dz(3, 256, 512)
+            quantize_x(3, 512, 768)
+            for v in range(6):
+                grad(v, 3)
+            quantize_x(3, 768, 1024)
+            for v in range(6, 8):
+                grad(v, 3)
+            for v in range(8):
+                finish(v, v % 2 == 1)

@@ -101,7 +101,7 @@ def tile_embedding_gradient_two_losses_s7_kernel(tc, ga, wa, gb, wb, lam, act, x
                 nc.scalar.activation(out=dst, in_=src, func=COPY, scale=sc)
 
         def interleave_x(g, c0, c1, on_scalar=False):
-            grp = wt("x_grp", [P, 512, 4], BF16, 4)
+            grp = wt("x_late", [P, 256, 4], BF16, 6) if c1 - c0 <= 256 else wt("x_grp", [P, 512, 4], BF16, 3)
             x_grp[g, c0] = grp
             (nc.scalar.copy if on_scalar else nc.vector.tensor_copy)(
                 out=grp[:, : c1 - c0, :].rearrange("p (c i) t -> p c t i", i=4),
@@ -118,7 +118,7 @@ def tile_embedding_gradient_two_losses_s7_kernel(tc, ga, wa, gb, wb, lam, act, x
         wa_grp = wt("sums", [P, 2, D, 4], BF16, 2)
         wa_codes = kt("wa_codes", [P, 2, D], U32)
         wa_scales = kt("wa_scales", [P, 2, D], U8)
-        wb_grp = wt("x_grp", [P, 512, 4], BF16, 4)
+        wb_grp = wt("x_grp", [P, 512, 4], BF16, 3)
         wb_codes = kt("wb_codes", [P, D], U32)
         wb_scales = kt("wb_scales", [P, D], U8)
 
@@ -127,8 +127,9 @@ def tile_embedding_gradient_two_losses_s7_kernel(tc, ga, wa, gb, wb, lam, act, x
                 for u in range(2):
                     nc.tensor.transpose(dst[:, c, u, :], words[:, 256 * c + u : 256 * (c + 1) : 2], ident[:])
 
-        def wa_turn(j):
+        def wa_turn(j, dummies=0):
             b = bank("tr")
+            warm(b, dummies)
             banks["wa", j] = b
             transpose_words(b[:].rearrange("p (c u r) -> p c u r", c=2, u=2), wa_sb[:, j, :].bitcast(F32), 2)
 
@@ -152,17 +153,24 @@ def tile_embedding_gradient_two_losses_s7_kernel(tc, ga, wa, gb, wb, lam, act, x
 
         banks = {}
 
-        def turn(s):
-            g, h = s // 2, s % 2
-            for i in range(2):
-                b = bank("tr")
-                banks[s, i] = b
-                transpose_words(b[:].rearrange("p (c u r) -> p c u r", c=2, u=2), ga_sb[g][:, 2 * h + i, :].bitcast(F32), 2)
+        warm_sb = kt("warm", [P, 512], BF16)
+        nc.vector.memset(warm_sb[:], 0.0)
+
+        def warm(b, n=1):
+            for i in range(n):
+                nc.tensor.matmul(b[:], lhsT=warm_sb[:, :P], rhs=warm_sb[:], start=True, stop=True)
+
+        def turn(k, dummies=0):
+            s, i = k // 2, k % 2
+            g, t = k // 4, k % 4
             b = bank("tr")
-            banks[s, 2] = b
-            bv = b[:].rearrange("p (i u r) -> p i u r", i=2, u=2)
-            for i in range(2):
-                transpose_words(bv[:, i : i + 1, :, :], gb_sb[g][:, 2 * h + i, :].bitcast(F32), 1)
+            banks[s, i] = b
+            warm(b, dummies)
+            transpose_words(b[:].rearrange("p (c u r) -> p c u r", c=2, u=2), ga_sb[g][:, t, :].bitcast(F32), 2)
+            if i == 0:
+                banks[s, 2] = bank("tr")
+            bv = banks[s, 2][:].rearrange("p (i u r) -> p i u r", i=2, u=2)
+            transpose_words(bv[:, i : i + 1, :, :], gb_sb[g][:, t, :].bitcast(F32), 1)
 
         def empty(s, i, on_vector=False):
             if i == 0:
@@ -243,9 +251,9 @@ def tile_embedding_gradient_two_losses_s7_kernel(tc, ga, wa, gb, wb, lam, act, x
             grp = wt("dz_grp", [P, 512, 4], BF16, 2)
             dz_grp[g, c0] = grp
             nc.vector.tensor_tensor(
-                out=grp[:, : c1 - c0, :].rearrange("p (c i) t -> p c t i", i=4),
-                in0=sums[g][:, :, c0:c1].rearrange("p t (c i) -> p c t i", i=4),
-                in1=act_sb[g][:, :, c0:c1].rearrange("p t (c i) -> p c t i", i=4),
+                out=grp[:, : c1 - c0, :].rearrange("p (c i) t -> p c t i", i=8),
+                in0=sums[g][:, :, c0:c1].rearrange("p t (c i) -> p c t i", i=8),
+                in1=act_sb[g][:, :, c0:c1].rearrange("p t (c i) -> p c t i", i=8),
                 op=MULT,
             )
 
@@ -280,13 +288,16 @@ def tile_embedding_gradient_two_losses_s7_kernel(tc, ga, wa, gb, wb, lam, act, x
         with tc.manual_schedule():
             W, S = True, False
             for t in range(4):
-                widen(0, t, 0, V, t != 3)
+                widen(0, t, 0, V, t != 1)
             for j in range(4):
-                wa_turn(j)
+                wa_turn(j, 12 if j == 0 else 1)
                 wa_empty(j)
             interleave_x(0, 0, 512)
-            turn(0)
-            empty(0, 0); empty(0, 1); empty(0, 2)
+            turn(0, 1)
+            empty(0, 0)
+            turn(1, 1)
+            empty(0, 1)
+            empty(0, 2)
             interleave_x(0, 512, 1024)
             quantize_wa(0)
             quantize_wa(1)
@@ -294,8 +305,11 @@ def tile_embedding_gradient_two_losses_s7_kernel(tc, ga, wa, gb, wb, lam, act, x
             quantize_a(0)
             quantize_wb()
             quantize_b(0)
-            turn(1)
-            empty(1, 0); empty(1, 1); empty(1, 2)
+            turn(2, 1)
+            empty(1, 0)
+            turn(3, 1)
+            empty(1, 1)
+            empty(1, 2)
             dve = {k: [] for k in range(20)}
             act = {k: [] for k in range(20)}
             for k in range(16):
@@ -326,15 +340,16 @@ def tile_embedding_gradient_two_losses_s7_kernel(tc, ga, wa, gb, wb, lam, act, x
             for k in range(16):
                 s = k // 2
                 products(k)
-                if k % 2 == 0 and s + 2 < 8:
-                    turn(s + 2)
                 if k >= 13:
                     grad(k - 13, 0)
                     grad(k - 13, 1)
+                if k + 4 < 16:
+                    turn(k + 4, 0)
                 weigh(k)
-                if s + 2 < 8:
-                    for i in ((0, 1) if k % 2 == 0 else (2,)):
-                        empty(s + 2, i)
+                if k + 4 < 16:
+                    empty(s + 2, k % 2)
+                    if k % 2 == 1:
+                        empty(s + 2, 2)
                 for f in act[k]:
                     f()
                 for f in dve[k]:

@@ -17,358 +17,374 @@ MULT = mybir.AluOpType.mult
 ADD = mybir.AluOpType.add
 
 P = 128
-G = T // 512
-PA_PASSES = CA // 512
+PACK = 4
+GROUP = P * PACK
+GROUPS = T // GROUP
+STEPS = GROUPS * PACK
+V_TILES = V // P
+
+BANKS = {"turned": 3, "head_a": 3, "head_b": 2}
+DE_BANKS = ["turned", "turned", "turned", "head_a", "head_b", "head_a", "head_b", "head_a"]
+
+WARM_FIRST, WARM_NEXT = 12, 1
+
+PLAN = {
+    0: [("pack_x", 0, 0, 512), ("widen", 1, 2, "vector"), ("widen", 1, 3, "vector"), ("pack_a", 1), ("widen", 1, 0, "scalar")],
+    1: [("pack_b", 1), ("widen", 1, 1, "vector"), ("pack_x", 0, 512, 1024), ("weave", 1, 0, 512, "vector")],
+    2: [("weave", 1, 512, 1024, "vector"), ("pack_a", 2), ("widen", 2, 1, "scalar")],
+    3: [("pack_x", 1, 0, 512), ("pack_b", 2), ("widen", 2, 0, "scalar")],
+    4: [("pack_a", 3), ("act", 0, 256, 512), ("pack_x", 1, 512, 1024), ("widen", 2, 3, "scalar"), ("pack_b", 3), ("act", 0, 0, 256)],
+    5: [("widen", 2, 2, "scalar")],
+    6: [("pack_dz", 0, 0, 512), ("pack_a", 4), ("pack_b", 4), ("weave", 2, 0, 512, "vector")],
+    7: [("weave", 2, 512, 1024, "vector"), ("widen", 3, 2, "scalar")],
+    8: [("pack_x", 2, 0, 512), ("widen", 3, 3, "scalar"), ("pack_a", 5), ("pack_b", 5)],
+    9: [("act", 1, 0, 256), ("act", 1, 256, 512)],
+    10: [("pack_b", 6), ("pack_a", 6)],
+    11: [("pack_dz", 1, 0, 512)],
+    12: [("pack_a", 7), ("pack_b", 7), ("act", 2, 256, 512)],
+    13: [("widen", 3, 0, "scalar")],
+    14: [("widen", 3, 1, "scalar")],
+    15: [("act", 2, 0, 256)],
+    17: [("pack_dz", 2, 0, 512), ("act", 3, 256, 512)],
+    20: [("pack_x", 2, 512, 1024)],
+    22: [("weave", 3, 768, 1024, "scalar"), ("act", 3, 0, 256), ("weave", 3, 512, 768, "scalar")],
+    23: [("pack_x", 3, 768, 1024), ("pack_dz", 3, 256, 512)],
+    24: [("pack_dz", 3, 0, 256)],
+    25: [("pack_x", 3, 512, 768)],
+    26: [("weave", 3, 0, 512, "vector"), ("pack_x", 3, 0, 512)],
+}
+EARLY_PASSES = {13: 3, 14: 1}
 
 
 def tile_embedding_gradient_two_losses_s7_kernel(tc, ga, wa, gb, wb, lam, act, x_bytes, x_scale, out):
     nc = tc.nc
     with ExitStack() as ctx:
         keep = ctx.enter_context(tc.tile_pool(name="keep", bufs=1))
-        work = ctx.enter_context(tc.tile_pool(name="work", bufs=2))
+        rotate = ctx.enter_context(tc.tile_pool(name="rotate", bufs=2))
         psum = ctx.enter_context(tc.psum_pool(name="psum", bufs=1))
 
-        def kt(name, shape, dt):
-            return keep.tile(shape, dt, name=name, tag=name, align_bytes=64)
+        def kept(name, shape, dtype):
+            return keep.tile(shape, dtype, name=name, tag=name, align_bytes=64)
 
-        def wt(name, shape, dt, bufs):
-            return work.tile(shape, dt, name=name, tag=name, bufs=bufs, align_bytes=64)
+        def rotated(tag, shape, dtype, bufs):
+            return rotate.tile(shape, dtype, name=tag, tag=tag, bufs=bufs, align_bytes=64)
 
-        def bank(tag):
-            return psum.tile([P, 512], F32, name="bank_" + tag, tag=tag, bufs={"tr": 3, "pa": 3, "pb": 2}[tag])
+        def bank(purpose):
+            return psum.tile([P, 512], F32, name=purpose, tag=purpose, bufs=BANKS[purpose])
 
-        xscale_sb = kt("xscale", [P, G, 4], F32)
-        nc.scalar.dma_start(out=xscale_sb[:], in_=x_scale.rearrange("(g p t) o -> p g (t o)", p=P, t=4))
-        lam_bf = kt("lam_bf", [P, G, 4], BF16)
-        nc.scalar.dma_start(out=lam_bf[:], in_=lam.rearrange("(g p t) -> p g t", p=P, t=4))
-
-        ident = kt("ident", [P, P], F32)
+        x_scale_sb = kept("x_scale_sb", [P, GROUPS, PACK], F32)
+        x_scale_view = x_scale.rearrange("(g p t) o -> p g (t o)", p=P, t=PACK)
+        nc.scalar.dma_start(out=x_scale_sb[:, 0, :], in_=x_scale_view[:, 0, :])
+        lam_raw = kept("lam_raw", [P, GROUPS, PACK], BF16)
+        ident = kept("ident", [P, P], F32)
         make_identity(nc, ident[:])
 
-        x_raw = [kt("x_raw%d" % g, [P, 4, V], U8) for g in range(G)]
-        x_view = x_bytes.rearrange("(g p t) n -> g p t n", p=P, t=4)
-        wa_sb = kt("wa_sb", [P, 4, CA], BF16)
+        x_raw = [kept("x_raw%d" % g, [P, PACK, V], U8) for g in range(GROUPS)]
+        wa_sb = kept("wa_sb", [P, D // P, CA], BF16)
+        wb_sb = kept("wb_sb", [P, PACK, D], BF16)
+        ga_sb = [kept("ga_sb%d" % g, [P, PACK, CA], BF16) for g in range(GROUPS)]
+        gb_sb = [kept("gb_sb%d" % g, [P, PACK, CB], BF16) for g in range(GROUPS)]
+        act_sb = [kept("act_sb%d" % g, [P, PACK, D], BF16) for g in range(GROUPS)]
+        x_view = x_bytes.rearrange("(g p t) v -> g p t v", p=P, t=PACK)
+        ga_view = ga.rearrange("(g p t) k -> g p t k", p=P, t=PACK)
+        gb_view = gb.rearrange("(g p t) k -> g p t k", p=P, t=PACK)
+        act_view = act.rearrange("(g p t) d -> g p t d", p=P, t=PACK)
         wa_view = wa.rearrange("(j r) k -> j r k", r=P)
-        wb_sb = kt("wb_sb", [P, 4, D], BF16)
-        ga_sb = [kt("ga_sb%d" % g, [P, 4, CA], BF16) for g in range(G)]
-        gb_sb = [kt("gb_sb%d" % g, [P, 4, CB], BF16) for g in range(G)]
-        act_sb = [kt("act_sb%d" % g, [P, 4, D], BF16) for g in range(G)]
-        ga_view = ga.rearrange("(g p t) k -> g p t k", p=P, t=4)
-        gb_view = gb.rearrange("(g p t) k -> g p t k", p=P, t=4)
-        act_view = act.rearrange("(g p t) k -> g p t k", p=P, t=4)
 
-        def load_x(g):
-            nc.sync.dma_start(out=x_raw[g][:], in_=x_view[g])
+        def load_pair(tile, view, s):
+            g, t = s // 2, 2 * (s % 2)
+            nc.sync.dma_start(out=tile[g][:, t : t + 2, :], in_=view[g][:, t : t + 2, :])
 
-        def load_pair(tile, view, h):
-            nc.sync.dma_start(out=tile[:, 2 * h : 2 * h + 2, :], in_=view[:, 2 * h : 2 * h + 2, :])
-
-        for t in range(4):
+        for t in range(PACK):
             nc.sync.dma_start(out=x_raw[0][:, t, :], in_=x_view[0][:, t, :])
-        for j in range(4):
+        for j in range(D // P):
             nc.sync.dma_start(out=wa_sb[:, j, :], in_=wa_view[j])
-        load_pair(ga_sb[0], ga_view[0], 0)
-        load_pair(gb_sb[0], gb_view[0], 0)
-        nc.sync.dma_start(out=wb_sb[:], in_=wb.rearrange("(p t) d -> p t d", t=4))
-        load_pair(ga_sb[0], ga_view[0], 1)
-        load_pair(gb_sb[0], gb_view[0], 1)
-        for g in range(1, G):
-            load_pair(ga_sb[g], ga_view[g], 0)
-            load_pair(gb_sb[g], gb_view[g], 0)
-            load_x(g)
-            load_pair(ga_sb[g], ga_view[g], 1)
-            load_pair(gb_sb[g], gb_view[g], 1)
+        load_pair(ga_sb, ga_view, 0)
+        load_pair(gb_sb, gb_view, 0)
+        nc.sync.dma_start(out=wb_sb[:], in_=wb.rearrange("(p j) d -> p j d", j=PACK))
+        load_pair(ga_sb, ga_view, 1)
+        load_pair(gb_sb, gb_view, 1)
+        nc.sync.dma_start(out=lam_raw[:], in_=lam.rearrange("(g p t) -> p g t", p=P, t=PACK))
+        nc.sync.dma_start(out=x_scale_sb[:, 1:, :], in_=x_scale_view[:, 1:, :])
+        nc.sync.dma_start(out=x_raw[1][:], in_=x_view[1])
+        for g in range(1, GROUPS):
+            load_pair(ga_sb, ga_view, 2 * g)
+            load_pair(gb_sb, gb_view, 2 * g)
             nc.sync.dma_start(out=act_sb[g - 1][:], in_=act_view[g - 1])
+            load_pair(ga_sb, ga_view, 2 * g + 1)
+            load_pair(gb_sb, gb_view, 2 * g + 1)
+            if g + 1 < GROUPS:
+                nc.sync.dma_start(out=x_raw[g + 1][:], in_=x_view[g + 1])
         nc.sync.dma_start(out=act_sb[3][:], in_=act_view[3])
 
-        lam_sb = kt("lam_sb", [P, G, 4], F32)
-        nc.gpsimd.tensor_copy(out=lam_sb[:], in_=lam_bf[:])
+        lam_sb = kept("lam_sb", [P, GROUPS, PACK], F32)
+        nc.gpsimd.tensor_copy(out=lam_sb[:], in_=lam_raw[:])
+        zeros = kept("zeros", [P, 512], BF16)
+        nc.vector.memset(zeros[:], 0.0)
 
-        x_codes = [kt("x_codes%d" % g, [P, V], U32) for g in range(G)]
-        x_scales = [kt("x_scales%d" % g, [P, V], U8) for g in range(G)]
-        x_wide = {}
-        x_grp = {}
+        x_codes = [kept("x_codes%d" % g, [P, V], U32) for g in range(GROUPS)]
+        x_scales = [kept("x_scales%d" % g, [P, V], U8) for g in range(GROUPS)]
+        dz_codes = [kept("dz_codes%d" % g, [P, D], U32) for g in range(GROUPS)]
+        dz_scales = [kept("dz_scales%d" % g, [P, D], U8) for g in range(GROUPS)]
+        wa_codes = kept("wa_codes", [P, CA // GROUP, D], U32)
+        wa_scales = kept("wa_scales", [P, CA // GROUP, D], U8)
+        wb_codes = kept("wb_codes", [P, D], U32)
+        wb_scales = kept("wb_scales", [P, D], U8)
 
-        def widen(g, t, c0, c1, on_vector):
+        def quantize(codes, scales, values):
+            nc.vector.quantize_mx(out=codes.bitcast(FP8X4), scales=scales, in_=values)
+
+        def product(acc, lhs, rhs, start, stop):
+            (lhs_codes, lhs_scales), (rhs_codes, rhs_scales) = lhs, rhs
+            nc.tensor.matmul_mx(
+                out=acc, lhsT=lhs_codes.bitcast(FP8X4), lhsT_scale=lhs_scales,
+                rhs=rhs_codes.bitcast(FP8X4), rhs_scale=rhs_scales, start=start, stop=stop,
+            )
+
+        x_wide, x_woven = {}, {}
+
+        def widen(g, t, engine):
             if g not in x_wide:
-                x_wide[g] = wt("x_wide", [P, 4, V], BF16, 3)
-            src = x_raw[g][:, t, c0:c1].bitcast(FP8)
-            dst = x_wide[g][:, t, c0:c1]
-            sc = xscale_sb[:, g, t : t + 1]
-            if on_vector:
-                nc.vector.tensor_scalar(out=dst, in0=src, scalar1=sc, scalar2=None, op0=MULT)
+                x_wide[g] = rotated("x_wide", [P, PACK, V], BF16, 3)
+            source = x_raw[g][:, t, :].bitcast(FP8)
+            scale = x_scale_sb[:, g, t : t + 1]
+            if engine == "vector":
+                nc.vector.tensor_scalar(out=x_wide[g][:, t, :], in0=source, scalar1=scale, scalar2=None, op0=MULT)
             else:
-                nc.scalar.activation(out=dst, in_=src, func=COPY, scale=sc)
+                nc.scalar.activation(out=x_wide[g][:, t, :], in_=source, func=COPY, scale=scale)
 
-        def interleave_x(g, c0, c1, on_scalar=False):
-            grp = wt("x_late", [P, 256, 4], BF16, 6) if c1 - c0 <= 256 else wt("x_grp", [P, 512, 4], BF16, 3)
-            x_grp[g, c0] = grp
-            (nc.scalar.copy if on_scalar else nc.vector.tensor_copy)(
-                out=grp[:, : c1 - c0, :].rearrange("p (c i) t -> p c t i", i=4),
-                in_=x_wide[g][:, :, c0:c1].rearrange("p t (c i) -> p c t i", i=4),
-            )
+        def weave_slots(dst, src, engine):
+            if engine == "vector":
+                nc.vector.tensor_copy(
+                    out=dst.rearrange("p (c i) t -> p c t i", i=4), in_=src.rearrange("p t (c i) -> p c t i", i=4)
+                )
+            else:
+                nc.scalar.copy(out=dst, in_=src.rearrange("p t c -> p c t"))
 
-        def quantize_x(g, c0, c1):
-            nc.vector.quantize_mx(
-                out=x_codes[g][:, c0:c1].bitcast(FP8X4),
-                scales=x_scales[g][:, c0:c1],
-                in_=x_grp[g, c0][:, : c1 - c0, :].rearrange("p n t -> p (n t)"),
-            )
+        def weave(g, c0, c1, engine):
+            if c1 - c0 == 512:
+                woven = rotated("woven_512", [P, 512, PACK], BF16, 4)
+            else:
+                woven = rotated("woven_256", [P, 256, PACK], BF16, 2)
+            x_woven[g, c0] = woven
+            weave_slots(woven[:], x_wide[g][:, :, c0:c1], engine)
 
-        wa_grp = wt("sums", [P, 2, D, 4], BF16, 2)
-        wa_codes = kt("wa_codes", [P, 2, D], U32)
-        wa_scales = kt("wa_scales", [P, 2, D], U8)
-        wb_grp = wt("x_grp", [P, 512, 4], BF16, 3)
-        wb_codes = kt("wb_codes", [P, D], U32)
-        wb_scales = kt("wb_scales", [P, D], U8)
+        def pack_x(g, c0, c1):
+            quantize(x_codes[g][:, c0:c1], x_scales[g][:, c0:c1], x_woven[g, c0][:].rearrange("p v t -> p (v t)"))
 
         def transpose_words(dst, words, passes):
             for c in range(passes):
                 for u in range(2):
                     nc.tensor.transpose(dst[:, c, u, :], words[:, 256 * c + u : 256 * (c + 1) : 2], ident[:])
 
-        def wa_turn(j, dummies=0):
-            b = bank("tr")
-            warm(b, dummies)
-            banks["wa", j] = b
-            transpose_words(b[:].rearrange("p (c u r) -> p c u r", c=2, u=2), wa_sb[:, j, :].bitcast(F32), 2)
+        def warm(acc, count):
+            for i in range(count):
+                nc.tensor.matmul(acc[:], lhsT=zeros[:, :P], rhs=zeros[:], start=True, stop=True)
 
-        def wa_empty(j):
-            bv = banks["wa", j][:].rearrange("p (c u r) -> p c u r", c=2, u=2)
+        def by_word(acc, n):
+            return acc[:].rearrange("p (n u r) -> p n u r", n=n, u=2)
+
+        turned = {}
+        wa_woven = rotated("sums", [P, CA // GROUP, D, PACK], BF16, 2)
+
+        def turn_wa(j):
+            acc = bank("turned")
+            warm(acc, WARM_FIRST if j == 0 else WARM_NEXT)
+            transpose_words(by_word(acc, 2), wa_sb[:, j, :].bitcast(F32), 2)
+            rows = wa_woven[:, :, P * j : P * (j + 1), :].rearrange("p c r j -> p c (r j)").bitcast(F32)
             nc.scalar.copy(
-                out=wa_grp[:, :, P * j : P * (j + 1), :].rearrange("p c r t -> p c (r t)").bitcast(F32).rearrange("p c (r u) -> p c r u", u=2),
-                in_=bv.rearrange("p c u r -> p c r u"),
+                out=rows.rearrange("p c (r u) -> p c r u", u=2), in_=by_word(acc, 2).rearrange("p c u r -> p c r u")
             )
 
-        def quantize_wa(c):
-            nc.vector.quantize_mx(out=wa_codes[:, c, :].bitcast(FP8X4), scales=wa_scales[:, c, :], in_=wa_grp[:, c, :, :].rearrange("p d t -> p (d t)"))
+        def pack_wa(c):
+            quantize(wa_codes[:, c, :], wa_scales[:, c, :], wa_woven[:, c, :, :].rearrange("p d j -> p (d j)"))
 
-        def interleave_wb():
-            nc.vector.tensor_copy(out=wb_grp[:].rearrange("p (c i) t -> p c t i", i=4), in_=wb_sb[:].rearrange("p t (c i) -> p c t i", i=4))
+        wb_woven = {}
 
-        def quantize_wb():
-            nc.vector.quantize_mx(out=wb_codes[:].bitcast(FP8X4), scales=wb_scales[:], in_=wb_grp[:].rearrange("p d t -> p (d t)"))
+        def weave_wb():
+            wb_woven[0] = rotated("woven_512", [P, D, PACK], BF16, 4)
+            weave_slots(wb_woven[0][:], wb_sb[:], "vector")
 
-        a_grp, b_grp, a_q, b_q = {}, {}, {}, {}
+        def pack_wb():
+            quantize(wb_codes[:], wb_scales[:], wb_woven[0][:].rearrange("p d j -> p (d j)"))
 
-        banks = {}
-
-        warm_sb = kt("warm", [P, 512], BF16)
-        nc.vector.memset(warm_sb[:], 0.0)
-
-        def warm(b, n=1):
-            for i in range(n):
-                nc.tensor.matmul(b[:], lhsT=warm_sb[:, :P], rhs=warm_sb[:], start=True, stop=True)
-
-        def turn(k, dummies=0):
+        def turn(k, warm_count):
             s, i = k // 2, k % 2
-            g, t = k // 4, k % 4
-            b = bank("tr")
-            banks[s, i] = b
-            warm(b, dummies)
-            transpose_words(b[:].rearrange("p (c u r) -> p c u r", c=2, u=2), ga_sb[g][:, t, :].bitcast(F32), 2)
+            acc = bank("turned")
+            turned[s, "a", i] = acc
+            warm(acc, warm_count)
+            transpose_words(by_word(acc, 2), ga_sb[k // PACK][:, k % PACK, :].bitcast(F32), CA // GROUP)
             if i == 0:
-                banks[s, 2] = bank("tr")
-            bv = banks[s, 2][:].rearrange("p (i u r) -> p i u r", i=2, u=2)
-            transpose_words(bv[:, i : i + 1, :, :], gb_sb[g][:, t, :].bitcast(F32), 1)
+                turned[s, "b"] = bank("turned")
+            transpose_words(
+                by_word(turned[s, "b"], 2)[:, i : i + 1, :, :], gb_sb[k // PACK][:, k % PACK, :].bitcast(F32), CB // GROUP
+            )
 
-        def empty(s, i, on_vector=False):
+        a_woven, b_woven, a_packed, b_packed = {}, {}, {}, {}
+
+        def empty(k):
+            s, i = k // 2, k % 2
             if i == 0:
-                a_grp[s] = wt("a_grp", [P, 2, 2, P, 4], BF16, 2)
-            if i == 2:
-                b_grp[s] = wt("b_grp", [P, 2, P, 4], BF16, 2)
-            if i < 2:
-                dst = a_grp[s][:, i, :, :, :].rearrange("p c r t -> p (c r t)")
-            else:
-                dst = b_grp[s][:].rearrange("p i r t -> p (i r t)")
-            dst = dst.bitcast(F32).rearrange("p (c r u) -> p c r u", c=2, u=2)
-            src = banks[s, i][:].rearrange("p (c u r) -> p c r u", c=2, u=2)
-            if on_vector:
-                nc.vector.tensor_copy(out=dst, in_=src)
-            else:
-                nc.scalar.copy(out=dst, in_=src)
+                a_woven[s] = rotated("a_woven", [P, 2, CA // GROUP, P, PACK], BF16, 2)
+            jobs = [(turned[s, "a", i], a_woven[s][:, i, :, :, :].rearrange("p c r j -> p (c r j)"))]
+            if i == 1:
+                b_woven[s] = rotated("b_woven", [P, 2, P, PACK], BF16, 2)
+                jobs.append((turned[s, "b"], b_woven[s][:].rearrange("p i r j -> p (i r j)")))
+            for acc, dst in jobs:
+                nc.scalar.copy(
+                    out=dst.bitcast(F32).rearrange("p (n r u) -> p n r u", n=2, u=2),
+                    in_=by_word(acc, 2).rearrange("p n u r -> p n r u"),
+                )
 
-        def quantize_a(s):
-            ac = wt("a_codes", [P, 2, 2, P], U32, 3)
-            asc = wt("a_scales", [P, 2, 2, P], U8, 3)
-            nc.vector.quantize_mx(
-                out=ac[:].rearrange("p i c r -> p (i c r)").bitcast(FP8X4),
-                scales=asc[:].rearrange("p i c r -> p (i c r)"),
-                in_=a_grp[s][:].rearrange("p i c r t -> p (i c r t)"),
+        def pack_a(s):
+            codes = rotated("a_codes", [P, 2, CA // GROUP, P], U32, 3)
+            scales = rotated("a_scales", [P, 2, CA // GROUP, P], U8, 3)
+            a_packed[s] = (codes, scales)
+            quantize(
+                codes[:].rearrange("p i c r -> p (i c r)"),
+                scales[:].rearrange("p i c r -> p (i c r)"),
+                a_woven[s][:].rearrange("p i c r j -> p (i c r j)"),
             )
-            a_q[s] = (ac, asc)
 
-        def quantize_b(s):
-            bc = wt("b_codes", [P, 2, P], U32, 3)
-            bsc = wt("b_scales", [P, 2, P], U8, 3)
-            nc.vector.quantize_mx(
-                out=bc[:].rearrange("p i r -> p (i r)").bitcast(FP8X4),
-                scales=bsc[:].rearrange("p i r -> p (i r)"),
-                in_=b_grp[s][:].rearrange("p i r t -> p (i r t)"),
+        def pack_b(s):
+            codes = rotated("b_codes", [P, 2, P], U32, 3)
+            scales = rotated("b_scales", [P, 2, P], U8, 3)
+            b_packed[s] = (codes, scales)
+            quantize(
+                codes[:].rearrange("p i r -> p (i r)"),
+                scales[:].rearrange("p i r -> p (i r)"),
+                b_woven[s][:].rearrange("p i r j -> p (i r j)"),
             )
-            b_q[s] = (bc, bsc)
 
-        pas, pbs = {}, {}
+        head_a, head_b, weighed, sums, dz_woven = {}, {}, {}, {}, {}
 
         def products(k):
             s, i = k // 2, k % 2
-            ac, asc = a_q[s]
-            bc, bsc = b_q[s]
-            pb = bank("pb")
-            nc.tensor.matmul_mx(
-                out=pb[:], lhsT=bc[:, i, :].bitcast(FP8X4), lhsT_scale=bsc[:, i, :],
-                rhs=wb_codes[:].bitcast(FP8X4), rhs_scale=wb_scales[:], start=True, stop=True,
-            )
-            pa = bank("pa")
-            for c in range(2):
-                nc.tensor.matmul_mx(
-                    out=pa[:], lhsT=ac[:, i, c, :].bitcast(FP8X4), lhsT_scale=asc[:, i, c, :],
-                    rhs=wa_codes[:, c, :].bitcast(FP8X4), rhs_scale=wa_scales[:, c, :], start=(c == 0), stop=(c == 1),
+            (a_codes, a_scales), (b_codes, b_scales) = a_packed[s], b_packed[s]
+            head_b[k] = bank("head_b")
+            product(head_b[k][:], (b_codes[:, i, :], b_scales[:, i, :]), (wb_codes[:], wb_scales[:]), True, True)
+            head_a[k] = bank("head_a")
+            for c in range(CA // GROUP):
+                product(
+                    head_a[k][:], (a_codes[:, i, c, :], a_scales[:, i, c, :]),
+                    (wa_codes[:, c, :], wa_scales[:, c, :]), c == 0, c == CA // GROUP - 1,
                 )
-            pas[k], pbs[k] = pa, pb
-
-        sums = {}
-
-        lam_pb = {}
 
         def weigh(k):
-            g, t = k // 4, k % 4
-            q = wt("row", [P, D], F32, 4)
-            lam_pb[k] = q
-            nc.scalar.activation(out=q[:], in_=pbs[k][:], func=COPY, scale=lam_sb[:, g, t : t + 1])
+            weighed[k] = rotated("weighed", [P, D], F32, 4)
+            lam_column = lam_sb[:, k // PACK, k % PACK : k % PACK + 1]
+            nc.scalar.activation(out=weighed[k][:], in_=head_b[k][:], func=COPY, scale=lam_column)
 
         def add(k):
-            g, t = k // 4, k % 4
+            g = k // PACK
             if g not in sums:
-                sums[g] = wt("sums", [P, 4, D], F32, 2)
-            nc.vector.tensor_tensor(out=sums[g][:, t, :], in0=pas[k][:], in1=lam_pb[k][:], op=ADD)
+                sums[g] = rotated("sums", [P, PACK, D], F32, 2)
+            nc.vector.tensor_tensor(out=sums[g][:, k % PACK, :], in0=head_a[k][:], in1=weighed[k][:], op=ADD)
 
-        dz_codes = [kt("dz_codes%d" % g, [P, D], U32) for g in range(G)]
-        dz_scales = [kt("dz_scales%d" % g, [P, D], U8) for g in range(G)]
-        dz_grp = {}
-
-        def times_act(g, c0, c1):
-            grp = wt("dz_grp", [P, 512, 4], BF16, 2)
-            dz_grp[g, c0] = grp
+        def act_product(g, c0, c1):
+            if g not in dz_woven:
+                dz_woven[g] = rotated("dz_woven", [P, D, PACK], BF16, 2)
             nc.vector.tensor_tensor(
-                out=grp[:, : c1 - c0, :].rearrange("p (c i) t -> p c t i", i=8),
+                out=dz_woven[g][:, c0:c1, :].rearrange("p (c i) t -> p c t i", i=8),
                 in0=sums[g][:, :, c0:c1].rearrange("p t (c i) -> p c t i", i=8),
                 in1=act_sb[g][:, :, c0:c1].rearrange("p t (c i) -> p c t i", i=8),
                 op=MULT,
             )
 
-        def quantize_dz(g, c0, c1):
-            nc.vector.quantize_mx(
-                out=dz_codes[g][:, c0:c1].bitcast(FP8X4), scales=dz_scales[g][:, c0:c1],
-                in_=dz_grp[g, c0][:, : c1 - c0, :].rearrange("p n t -> p (n t)"),
+        def pack_dz(g, c0, c1):
+            quantize(
+                dz_codes[g][:, c0:c1], dz_scales[g][:, c0:c1], dz_woven[g][:, c0:c1, :].rearrange("p d t -> p (d t)")
             )
 
-        tags = ["tr", "tr", "tr", "pa", "pb", "pa", "pb", "pa"]
-        accs = {}
+        de, passes_done, finished, packed = {}, [0] * V_TILES, [], set()
 
-        def grad(v, g):
-            if v not in accs:
-                accs[v] = bank(tags[v])
-            cols = slice(P * v, P * (v + 1))
-            nc.tensor.matmul_mx(
-                out=accs[v][:], lhsT=x_codes[g][:, cols].bitcast(FP8X4), lhsT_scale=x_scales[g][:, cols],
-                rhs=dz_codes[g][:].bitcast(FP8X4), rhs_scale=dz_scales[g][:], start=(g == 0), stop=(g == G - 1),
+        def is_ready(v, g):
+            needs = [("x", g, P * v), ("dz", g, 0), ("dz", g, D - 1)]
+            return all(any(n == m and h == g and c0 <= c < c1 for m, h, c0, c1 in packed) for n, g, c in needs)
+
+        def one_pass(v):
+            g = passes_done[v]
+            if g == 0:
+                de[v] = bank(DE_BANKS[v])
+            columns = slice(P * v, P * (v + 1))
+            product(
+                de[v][:], (x_codes[g][:, columns], x_scales[g][:, columns]),
+                (dz_codes[g][:], dz_scales[g][:]), g == 0, g == GROUPS - 1,
             )
+            passes_done[v] += 1
 
-        def finish(v, on_vector):
-            if v % 4 == 0:
-                sums["out", v // 4] = wt("sums", [P, 4, D], F32, 2)
-            res = sums["out", v // 4][:, v % 4, :]
-            if on_vector:
-                nc.vector.tensor_copy(out=res, in_=accs[v][:])
+        def finish(v):
+            n = len(finished)
+            finished.append(v)
+            if n % PACK == 0:
+                sums["out", n // PACK] = rotated("sums", [P, PACK, D], F32, 2)
+            result = sums["out", n // PACK][:, n % PACK, :]
+            if n in (4, 6):
+                nc.vector.tensor_copy(out=result, in_=de[v][:])
             else:
-                nc.scalar.copy(out=res, in_=accs[v][:])
-            nc.sync.dma_start(out=out[P * v : P * (v + 1), :], in_=res)
+                nc.scalar.copy(out=result, in_=de[v][:])
+            nc.sync.dma_start(out=out[P * v : P * (v + 1), :], in_=result)
+
+        def follow_plan(k):
+            for item in PLAN.get(k, []):
+                what, args = item[0], item[1:]
+                if what == "widen":
+                    widen(*args)
+                elif what == "weave":
+                    weave(*args)
+                elif what == "pack_x":
+                    pack_x(*args)
+                    packed.add(("x", args[0], args[1], args[2]))
+                elif what == "pack_a":
+                    pack_a(*args)
+                elif what == "pack_b":
+                    pack_b(*args)
+                elif what == "act":
+                    act_product(*args)
+                else:
+                    pack_dz(*args)
+                    packed.add(("dz", args[0], args[1], args[2]))
 
         with tc.manual_schedule():
-            W, S = True, False
-            for t in range(4):
-                widen(0, t, 0, V, t != 1)
-            for j in range(4):
-                wa_turn(j, 12 if j == 0 else 1)
-                wa_empty(j)
-            interleave_x(0, 0, 512)
-            turn(0, 1)
-            empty(0, 0)
-            turn(1, 1)
-            empty(0, 1)
-            empty(0, 2)
-            interleave_x(0, 512, 1024)
-            quantize_wa(0)
-            quantize_wa(1)
-            interleave_wb()
-            quantize_a(0)
-            quantize_wb()
-            quantize_b(0)
-            turn(2, 1)
-            empty(1, 0)
-            turn(3, 1)
-            empty(1, 1)
-            empty(1, 2)
-            dve = {k: [] for k in range(20)}
-            act = {k: [] for k in range(20)}
-            for k in range(16):
-                s = k // 2
-                if k % 2 == 0 and s + 1 < 8:
-                    dve[k].append(lambda s=s: quantize_a(s + 1))
-                    dve[k].append(lambda s=s: quantize_b(s + 1))
-            dve[0].insert(0, lambda: quantize_x(0, 0, 512))
-            dve[1].insert(0, lambda: quantize_x(0, 512, 1024))
-            for i in range(4):
-                dve[1 + i // 2].append(lambda i=i: widen(1, i, 0, V, W))
-                act[4 + i].append(lambda i=i: widen(2, i, 0, V, S))
-                act[8 + i].append(lambda i=i: widen(3, i, 0, V, S))
-                act[12 + i].append(lambda i=i: interleave_x(3, 256 * i, 256 * i + 256, True))
-            for i, c in enumerate((0, 512)):
-                dve[3 + i].append(lambda c=c: interleave_x(1, c, c + 512))
-                dve[4 + 2 * i].insert(0, lambda c=c: quantize_x(1, c, c + 512))
-                dve[9 + 2 * i].append(lambda c=c: interleave_x(2, c, c + 512))
-                dve[10 + 2 * i].append(lambda c=c: quantize_x(2, c, c + 512))
-            for g in range(3):
-                dve[4 * g + 4].append(lambda g=g: times_act(g, 0, 256))
-                dve[4 * g + 5].append(lambda g=g: times_act(g, 256, 512))
-                dve[4 * g + 5].append(lambda g=g: quantize_dz(g, 0, 256))
-                dve[4 * g + 6].append(lambda g=g: quantize_dz(g, 256, 512))
-            dve[14].append(lambda: quantize_x(3, 0, 256))
-            dve[15].append(lambda: quantize_x(3, 256, 512))
+            for t in range(PACK):
+                widen(0, t, "scalar" if t == 3 else "vector")
+            for j in range(D // P):
+                turn_wa(j)
+            weave(0, 0, 512, "vector")
+            for k in (0, 1):
+                turn(k, WARM_NEXT)
+                empty(k)
+            weave(0, 512, 1024, "vector")
+            pack_wa(0)
+            pack_wa(1)
+            weave_wb()
+            pack_a(0)
+            pack_wb()
+            pack_b(0)
+            for k in (2, 3):
+                turn(k, WARM_NEXT)
+                empty(k)
 
-            for k in range(16):
-                s = k // 2
+            for k in range(STEPS):
                 products(k)
-                if k >= 13:
-                    grad(k - 13, 0)
-                    grad(k - 13, 1)
-                if k + 4 < 16:
-                    turn(k + 4, 0)
+                for i in range(EARLY_PASSES.get(k, 0)):
+                    ready = [v for v in range(BANKS["turned"]) if passes_done[v] < GROUPS and is_ready(v, passes_done[v])]
+                    if ready:
+                        one_pass(ready[0])
+                if k + PACK < STEPS:
+                    turn(k + PACK, 0)
                 weigh(k)
-                if k + 4 < 16:
-                    empty(s + 2, k % 2)
-                    if k % 2 == 1:
-                        empty(s + 2, 2)
-                for f in act[k]:
-                    f()
-                for f in dve[k]:
-                    f()
+                if k + PACK < STEPS:
+                    empty(k + PACK)
+                follow_plan(k)
                 add(k)
-            for v in range(3):
-                grad(v, 2)
-            for v in range(3, 8):
-                for g in range(3):
-                    grad(v, g)
-            times_act(3, 0, 256)
-            times_act(3, 256, 512)
-            quantize_dz(3, 0, 256)
-            quantize_dz(3, 256, 512)
-            quantize_x(3, 512, 768)
-            for v in range(6):
-                grad(v, 3)
-            quantize_x(3, 768, 1024)
-            for v in range(6, 8):
-                grad(v, 3)
-            for v in range(8):
-                finish(v, v % 2 == 1)
+
+            for k in range(STEPS, max(PLAN) + 2):
+                for g in range(GROUPS):
+                    for v in range(V_TILES):
+                        if passes_done[v] == g and is_ready(v, g):
+                            one_pass(v)
+                for v in range(V_TILES):
+                    if passes_done[v] == GROUPS and v not in finished:
+                        finish(v)
+                follow_plan(k)

from contextlib import ExitStack

import concourse.mybir as mybir
from concourse.masks import make_identity

T, V, D, CA, CB = 2048, 1024, 512, 1024, 512
FLOPS = 2 * T * D * CA + 2 * T * D * CB + 2 * V * D * T

F32 = mybir.dt.float32
BF16 = mybir.dt.bfloat16
U32 = mybir.dt.uint32
U8 = mybir.dt.uint8
FP8 = mybir.dt.float8_e4m3fn
FP8X4 = mybir.dt.float8_e4m3fn_x4
COPY = mybir.ActivationFunctionType.Copy
MULT = mybir.AluOpType.mult
ADD = mybir.AluOpType.add

P = 128
PACK = 4
GROUP = P * PACK
GROUPS = T // GROUP
STEPS = GROUPS * PACK
V_TILES = V // P

BANKS = {"turned": 3, "head_a": 3, "head_b": 2}
DE_BANKS = ["turned", "turned", "turned", "head_a", "head_b", "head_a", "head_b", "head_a"]

WARM_FIRST, WARM_NEXT = 12, 1

PLAN = {
    0: [("pack_x", 0, 0, 512), ("widen", 1, 2, "vector"), ("widen", 1, 3, "vector"), ("pack_a", 1), ("widen", 1, 0, "scalar")],
    1: [("pack_b", 1), ("widen", 1, 1, "vector"), ("pack_x", 0, 512, 1024), ("weave", 1, 0, 512, "vector")],
    2: [("weave", 1, 512, 1024, "vector"), ("pack_a", 2), ("widen", 2, 1, "scalar")],
    3: [("pack_x", 1, 0, 512), ("pack_b", 2), ("widen", 2, 0, "scalar")],
    4: [("pack_a", 3), ("act", 0, 256, 512), ("pack_x", 1, 512, 1024), ("widen", 2, 3, "scalar"), ("pack_b", 3), ("act", 0, 0, 256)],
    5: [("widen", 2, 2, "scalar")],
    6: [("pack_dz", 0, 0, 512), ("pack_a", 4), ("pack_b", 4), ("weave", 2, 0, 512, "vector")],
    7: [("weave", 2, 512, 1024, "vector"), ("widen", 3, 2, "scalar")],
    8: [("pack_x", 2, 0, 512), ("widen", 3, 3, "scalar"), ("pack_a", 5), ("pack_b", 5)],
    9: [("act", 1, 0, 256), ("act", 1, 256, 512)],
    10: [("pack_b", 6), ("pack_a", 6)],
    11: [("pack_dz", 1, 0, 512)],
    12: [("pack_a", 7), ("pack_b", 7), ("act", 2, 256, 512)],
    13: [("widen", 3, 0, "scalar")],
    14: [("widen", 3, 1, "scalar")],
    15: [("act", 2, 0, 256)],
    17: [("pack_dz", 2, 0, 512), ("act", 3, 256, 512)],
    20: [("pack_x", 2, 512, 1024)],
    22: [("weave", 3, 768, 1024, "scalar"), ("act", 3, 0, 256), ("weave", 3, 512, 768, "scalar")],
    23: [("pack_x", 3, 768, 1024), ("pack_dz", 3, 256, 512)],
    24: [("pack_dz", 3, 0, 256)],
    25: [("pack_x", 3, 512, 768)],
    26: [("weave", 3, 0, 512, "vector"), ("pack_x", 3, 0, 512)],
}
EARLY_PASSES = {13: 3, 14: 1}


def tile_embedding_gradient_two_losses_s7_kernel(tc, ga, wa, gb, wb, lam, act, x_bytes, x_scale, out):
    nc = tc.nc
    with ExitStack() as ctx:
        keep = ctx.enter_context(tc.tile_pool(name="keep", bufs=1))
        rotate = ctx.enter_context(tc.tile_pool(name="rotate", bufs=2))
        psum = ctx.enter_context(tc.psum_pool(name="psum", bufs=1))

        def kept(name, shape, dtype):
            return keep.tile(shape, dtype, name=name, tag=name, align_bytes=64)

        def rotated(tag, shape, dtype, bufs):
            return rotate.tile(shape, dtype, name=tag, tag=tag, bufs=bufs, align_bytes=64)

        def bank(purpose):
            return psum.tile([P, 512], F32, name=purpose, tag=purpose, bufs=BANKS[purpose])

        x_scale_sb = kept("x_scale_sb", [P, GROUPS, PACK], F32)
        x_scale_view = x_scale.rearrange("(g p t) o -> p g (t o)", p=P, t=PACK)
        nc.scalar.dma_start(out=x_scale_sb[:, 0, :], in_=x_scale_view[:, 0, :])
        lam_raw = kept("lam_raw", [P, GROUPS, PACK], BF16)
        ident = kept("ident", [P, P], F32)
        make_identity(nc, ident[:])

        x_raw = [kept("x_raw%d" % g, [P, PACK, V], U8) for g in range(GROUPS)]
        wa_sb = kept("wa_sb", [P, D // P, CA], BF16)
        wb_sb = kept("wb_sb", [P, PACK, D], BF16)
        ga_sb = [kept("ga_sb%d" % g, [P, PACK, CA], BF16) for g in range(GROUPS)]
        gb_sb = [kept("gb_sb%d" % g, [P, PACK, CB], BF16) for g in range(GROUPS)]
        act_sb = [kept("act_sb%d" % g, [P, PACK, D], BF16) for g in range(GROUPS)]
        x_view = x_bytes.rearrange("(g p t) v -> g p t v", p=P, t=PACK)
        ga_view = ga.rearrange("(g p t) k -> g p t k", p=P, t=PACK)
        gb_view = gb.rearrange("(g p t) k -> g p t k", p=P, t=PACK)
        act_view = act.rearrange("(g p t) d -> g p t d", p=P, t=PACK)
        wa_view = wa.rearrange("(j r) k -> j r k", r=P)

        def load_pair(tile, view, s):
            g, t = s // 2, 2 * (s % 2)
            nc.sync.dma_start(out=tile[g][:, t : t + 2, :], in_=view[g][:, t : t + 2, :])

        for t in range(PACK):
            nc.sync.dma_start(out=x_raw[0][:, t, :], in_=x_view[0][:, t, :])
        for j in range(D // P):
            nc.sync.dma_start(out=wa_sb[:, j, :], in_=wa_view[j])
        load_pair(ga_sb, ga_view, 0)
        load_pair(gb_sb, gb_view, 0)
        nc.sync.dma_start(out=wb_sb[:], in_=wb.rearrange("(p j) d -> p j d", j=PACK))
        load_pair(ga_sb, ga_view, 1)
        load_pair(gb_sb, gb_view, 1)
        nc.sync.dma_start(out=lam_raw[:], in_=lam.rearrange("(g p t) -> p g t", p=P, t=PACK))
        nc.sync.dma_start(out=x_scale_sb[:, 1:, :], in_=x_scale_view[:, 1:, :])
        nc.sync.dma_start(out=x_raw[1][:], in_=x_view[1])
        for g in range(1, GROUPS):
            load_pair(ga_sb, ga_view, 2 * g)
            load_pair(gb_sb, gb_view, 2 * g)
            nc.sync.dma_start(out=act_sb[g - 1][:], in_=act_view[g - 1])
            load_pair(ga_sb, ga_view, 2 * g + 1)
            load_pair(gb_sb, gb_view, 2 * g + 1)
            if g + 1 < GROUPS:
                nc.sync.dma_start(out=x_raw[g + 1][:], in_=x_view[g + 1])
        nc.sync.dma_start(out=act_sb[3][:], in_=act_view[3])

        lam_sb = kept("lam_sb", [P, GROUPS, PACK], F32)
        nc.gpsimd.tensor_copy(out=lam_sb[:], in_=lam_raw[:])
        zeros = kept("zeros", [P, 512], BF16)
        nc.vector.memset(zeros[:], 0.0)

        x_codes = [kept("x_codes%d" % g, [P, V], U32) for g in range(GROUPS)]
        x_scales = [kept("x_scales%d" % g, [P, V], U8) for g in range(GROUPS)]
        dz_codes = [kept("dz_codes%d" % g, [P, D], U32) for g in range(GROUPS)]
        dz_scales = [kept("dz_scales%d" % g, [P, D], U8) for g in range(GROUPS)]
        wa_codes = kept("wa_codes", [P, CA // GROUP, D], U32)
        wa_scales = kept("wa_scales", [P, CA // GROUP, D], U8)
        wb_codes = kept("wb_codes", [P, D], U32)
        wb_scales = kept("wb_scales", [P, D], U8)

        def quantize(codes, scales, values):
            nc.vector.quantize_mx(out=codes.bitcast(FP8X4), scales=scales, in_=values)

        def product(acc, lhs, rhs, start, stop):
            (lhs_codes, lhs_scales), (rhs_codes, rhs_scales) = lhs, rhs
            nc.tensor.matmul_mx(
                out=acc, lhsT=lhs_codes.bitcast(FP8X4), lhsT_scale=lhs_scales,
                rhs=rhs_codes.bitcast(FP8X4), rhs_scale=rhs_scales, start=start, stop=stop,
            )

        x_wide, x_woven = {}, {}

        def widen(g, t, engine):
            if g not in x_wide:
                x_wide[g] = rotated("x_wide", [P, PACK, V], BF16, 3)
            source = x_raw[g][:, t, :].bitcast(FP8)
            scale = x_scale_sb[:, g, t : t + 1]
            if engine == "vector":
                nc.vector.tensor_scalar(out=x_wide[g][:, t, :], in0=source, scalar1=scale, scalar2=None, op0=MULT)
            else:
                nc.scalar.activation(out=x_wide[g][:, t, :], in_=source, func=COPY, scale=scale)

        def weave_slots(dst, src, engine):
            if engine == "vector":
                nc.vector.tensor_copy(
                    out=dst.rearrange("p (c i) t -> p c t i", i=4), in_=src.rearrange("p t (c i) -> p c t i", i=4)
                )
            else:
                nc.scalar.copy(out=dst, in_=src.rearrange("p t c -> p c t"))

        def weave(g, c0, c1, engine):
            if c1 - c0 == 512:
                woven = rotated("woven_512", [P, 512, PACK], BF16, 4)
            else:
                woven = rotated("woven_256", [P, 256, PACK], BF16, 2)
            x_woven[g, c0] = woven
            weave_slots(woven[:], x_wide[g][:, :, c0:c1], engine)

        def pack_x(g, c0, c1):
            quantize(x_codes[g][:, c0:c1], x_scales[g][:, c0:c1], x_woven[g, c0][:].rearrange("p v t -> p (v t)"))

        def transpose_words(dst, words, passes):
            for c in range(passes):
                for u in range(2):
                    nc.tensor.transpose(dst[:, c, u, :], words[:, 256 * c + u : 256 * (c + 1) : 2], ident[:])

        def warm(acc, count):
            for i in range(count):
                nc.tensor.matmul(acc[:], lhsT=zeros[:, :P], rhs=zeros[:], start=True, stop=True)

        def by_word(acc, n):
            return acc[:].rearrange("p (n u r) -> p n u r", n=n, u=2)

        turned = {}
        wa_woven = rotated("sums", [P, CA // GROUP, D, PACK], BF16, 2)

        def turn_wa(j):
            acc = bank("turned")
            warm(acc, WARM_FIRST if j == 0 else WARM_NEXT)
            transpose_words(by_word(acc, 2), wa_sb[:, j, :].bitcast(F32), 2)
            rows = wa_woven[:, :, P * j : P * (j + 1), :].rearrange("p c r j -> p c (r j)").bitcast(F32)
            nc.scalar.copy(
                out=rows.rearrange("p c (r u) -> p c r u", u=2), in_=by_word(acc, 2).rearrange("p c u r -> p c r u")
            )

        def pack_wa(c):
            quantize(wa_codes[:, c, :], wa_scales[:, c, :], wa_woven[:, c, :, :].rearrange("p d j -> p (d j)"))

        wb_woven = {}

        def weave_wb():
            wb_woven[0] = rotated("woven_512", [P, D, PACK], BF16, 4)
            weave_slots(wb_woven[0][:], wb_sb[:], "vector")

        def pack_wb():
            quantize(wb_codes[:], wb_scales[:], wb_woven[0][:].rearrange("p d j -> p (d j)"))

        def turn(k, warm_count):
            s, i = k // 2, k % 2
            acc = bank("turned")
            turned[s, "a", i] = acc
            warm(acc, warm_count)
            transpose_words(by_word(acc, 2), ga_sb[k // PACK][:, k % PACK, :].bitcast(F32), CA // GROUP)
            if i == 0:
                turned[s, "b"] = bank("turned")
            transpose_words(
                by_word(turned[s, "b"], 2)[:, i : i + 1, :, :], gb_sb[k // PACK][:, k % PACK, :].bitcast(F32), CB // GROUP
            )

        a_woven, b_woven, a_packed, b_packed = {}, {}, {}, {}

        def empty(k):
            s, i = k // 2, k % 2
            if i == 0:
                a_woven[s] = rotated("a_woven", [P, 2, CA // GROUP, P, PACK], BF16, 2)
            jobs = [(turned[s, "a", i], a_woven[s][:, i, :, :, :].rearrange("p c r j -> p (c r j)"))]
            if i == 1:
                b_woven[s] = rotated("b_woven", [P, 2, P, PACK], BF16, 2)
                jobs.append((turned[s, "b"], b_woven[s][:].rearrange("p i r j -> p (i r j)")))
            for acc, dst in jobs:
                nc.scalar.copy(
                    out=dst.bitcast(F32).rearrange("p (n r u) -> p n r u", n=2, u=2),
                    in_=by_word(acc, 2).rearrange("p n u r -> p n r u"),
                )

        def pack_a(s):
            codes = rotated("a_codes", [P, 2, CA // GROUP, P], U32, 3)
            scales = rotated("a_scales", [P, 2, CA // GROUP, P], U8, 3)
            a_packed[s] = (codes, scales)
            quantize(
                codes[:].rearrange("p i c r -> p (i c r)"),
                scales[:].rearrange("p i c r -> p (i c r)"),
                a_woven[s][:].rearrange("p i c r j -> p (i c r j)"),
            )

        def pack_b(s):
            codes = rotated("b_codes", [P, 2, P], U32, 3)
            scales = rotated("b_scales", [P, 2, P], U8, 3)
            b_packed[s] = (codes, scales)
            quantize(
                codes[:].rearrange("p i r -> p (i r)"),
                scales[:].rearrange("p i r -> p (i r)"),
                b_woven[s][:].rearrange("p i r j -> p (i r j)"),
            )

        head_a, head_b, weighed, sums, dz_woven = {}, {}, {}, {}, {}

        def products(k):
            s, i = k // 2, k % 2
            (a_codes, a_scales), (b_codes, b_scales) = a_packed[s], b_packed[s]
            head_b[k] = bank("head_b")
            product(head_b[k][:], (b_codes[:, i, :], b_scales[:, i, :]), (wb_codes[:], wb_scales[:]), True, True)
            head_a[k] = bank("head_a")
            for c in range(CA // GROUP):
                product(
                    head_a[k][:], (a_codes[:, i, c, :], a_scales[:, i, c, :]),
                    (wa_codes[:, c, :], wa_scales[:, c, :]), c == 0, c == CA // GROUP - 1,
                )

        def weigh(k):
            weighed[k] = rotated("weighed", [P, D], F32, 4)
            lam_column = lam_sb[:, k // PACK, k % PACK : k % PACK + 1]
            nc.scalar.activation(out=weighed[k][:], in_=head_b[k][:], func=COPY, scale=lam_column)

        def add(k):
            g = k // PACK
            if g not in sums:
                sums[g] = rotated("sums", [P, PACK, D], F32, 2)
            nc.vector.tensor_tensor(out=sums[g][:, k % PACK, :], in0=head_a[k][:], in1=weighed[k][:], op=ADD)

        def act_product(g, c0, c1):
            if g not in dz_woven:
                dz_woven[g] = rotated("dz_woven", [P, D, PACK], BF16, 2)
            nc.vector.tensor_tensor(
                out=dz_woven[g][:, c0:c1, :].rearrange("p (c i) t -> p c t i", i=8),
                in0=sums[g][:, :, c0:c1].rearrange("p t (c i) -> p c t i", i=8),
                in1=act_sb[g][:, :, c0:c1].rearrange("p t (c i) -> p c t i", i=8),
                op=MULT,
            )

        def pack_dz(g, c0, c1):
            quantize(
                dz_codes[g][:, c0:c1], dz_scales[g][:, c0:c1], dz_woven[g][:, c0:c1, :].rearrange("p d t -> p (d t)")
            )

        de, passes_done, finished, packed = {}, [0] * V_TILES, [], set()

        def is_ready(v, g):
            needs = [("x", g, P * v), ("dz", g, 0), ("dz", g, D - 1)]
            return all(any(n == m and h == g and c0 <= c < c1 for m, h, c0, c1 in packed) for n, g, c in needs)

        def one_pass(v):
            g = passes_done[v]
            if g == 0:
                de[v] = bank(DE_BANKS[v])
            columns = slice(P * v, P * (v + 1))
            product(
                de[v][:], (x_codes[g][:, columns], x_scales[g][:, columns]),
                (dz_codes[g][:], dz_scales[g][:]), g == 0, g == GROUPS - 1,
            )
            passes_done[v] += 1

        def finish(v):
            n = len(finished)
            finished.append(v)
            if n % PACK == 0:
                sums["out", n // PACK] = rotated("sums", [P, PACK, D], F32, 2)
            result = sums["out", n // PACK][:, n % PACK, :]
            if n in (4, 6):
                nc.vector.tensor_copy(out=result, in_=de[v][:])
            else:
                nc.scalar.copy(out=result, in_=de[v][:])
            nc.sync.dma_start(out=out[P * v : P * (v + 1), :], in_=result)

        def follow_plan(k):
            for item in PLAN.get(k, []):
                what, args = item[0], item[1:]
                if what == "widen":
                    widen(*args)
                elif what == "weave":
                    weave(*args)
                elif what == "pack_x":
                    pack_x(*args)
                    packed.add(("x", args[0], args[1], args[2]))
                elif what == "pack_a":
                    pack_a(*args)
                elif what == "pack_b":
                    pack_b(*args)
                elif what == "act":
                    act_product(*args)
                else:
                    pack_dz(*args)
                    packed.add(("dz", args[0], args[1], args[2]))

        with tc.manual_schedule():
            for t in range(PACK):
                widen(0, t, "scalar" if t == 3 else "vector")
            for j in range(D // P):
                turn_wa(j)
            weave(0, 0, 512, "vector")
            for k in (0, 1):
                turn(k, WARM_NEXT)
                empty(k)
            weave(0, 512, 1024, "vector")
            pack_wa(0)
            pack_wa(1)
            weave_wb()
            pack_a(0)
            pack_wb()
            pack_b(0)
            for k in (2, 3):
                turn(k, WARM_NEXT)
                empty(k)

            for k in range(STEPS):
                products(k)
                for i in range(EARLY_PASSES.get(k, 0)):
                    ready = [v for v in range(BANKS["turned"]) if passes_done[v] < GROUPS and is_ready(v, passes_done[v])]
                    if ready:
                        one_pass(ready[0])
                if k + PACK < STEPS:
                    turn(k + PACK, 0)
                weigh(k)
                if k + PACK < STEPS:
                    empty(k + PACK)
                follow_plan(k)
                add(k)

            for k in range(STEPS, max(PLAN) + 2):
                for g in range(GROUPS):
                    for v in range(V_TILES):
                        if passes_done[v] == g and is_ready(v, g):
                            one_pass(v)
                for v in range(V_TILES):
                    if passes_done[v] == GROUPS and v not in finished:
                        finish(v)
                follow_plan(k)
